import numpy as np
import ml_dtypes


def mxq(x, axis, fmt="e4m3"):
    dtype, down = {"e4m3": (ml_dtypes.float8_e4m3fn, 7), "e5m2": (ml_dtypes.float8_e5m2, 14)}[fmt]
    v = np.moveaxis(np.asarray(x, np.float32).astype(ml_dtypes.bfloat16).astype(np.float64), axis, -1)
    blocks = v.reshape(v.shape[:-1] + (-1, 32))
    amax = np.abs(blocks).max(-1, keepdims=True)
    byte = np.maximum(np.where(amax > 0, np.frexp(amax)[1] - 1 + 127, 0) - down, 1)
    scale = np.exp2(byte - 127.0)
    codes = (blocks / scale).astype(np.float32).astype(dtype).astype(np.float64)
    return np.moveaxis((codes * scale).reshape(v.shape), -1, axis)


WIDE = False


def mx_kscale(k, group=512):
    if not WIDE:
        return np.ones(k)
    levels = np.array([18, -18])
    if group != 512:
        return np.exp2(np.random.permutation(np.resize(levels, k // group))).repeat(group)
    if k % 512:
        return np.exp2(np.random.permutation(np.resize(levels, k // 32))).repeat(32)
    a = np.empty((k // 512, 16))
    for p in range(k // 512):
        a[p, :8] = np.random.permutation(np.resize(levels, 8))
        for g in range(8):
            far = levels[np.abs(levels - a[p, g]) >= 10]
            a[p, g + 8] = far[np.random.randint(len(far))]
    return np.exp2(a.ravel()).repeat(32)


def f64(x):
    return np.asarray(x).astype(np.float64)


G, D, M, N = 8, 128, 128, 512


def setup_inputs():
    n = np.random.standard_normal
    s = mx_kscale(D, 0)[:, None]
    return {
        "x": (n((G, D, N)) * s).astype(np.float32),
        "w": (n((G, D, M)) / np.sqrt(D) / s).astype(np.float32),
        "r": n((G, M, N)).astype(np.float32),
    }


def reference(x, w, r):
    xq = mxq(f64(x), 1, "e4m3")
    y = mxq(f64(w), 1, "e4m3").transpose(0, 2, 1) @ xq
    y = np.maximum(y, 0.0)
    y = y + f64(r)
    return y

@@ -1,0 +1,112 @@
+from contextlib import ExitStack
+
+import concourse.mybir as mybir
+
+G, D, M, N = 8, 128, 128, 512
+FLOPS = 2 * G * D * M * N
+
+F32 = mybir.dt.float32
+BF16 = mybir.dt.bfloat16
+U32 = mybir.dt.uint32
+U8 = mybir.dt.uint8
+FP8X4 = mybir.dt.float8_e4m3fn_x4
+ALU = mybir.AluOpType
+
+P = 128
+PACK = 4
+ROWS = D // PACK
+SIDE = P // ROWS
+SETS = G // SIDE
+PAIR = 2
+X_SPLIT = 352
+
+
+def interleave(copy, dst, src):
+    copy(
+        out=dst.rearrange("p (c i) j -> p c j i", i=4),
+        in_=src.rearrange("p j (c i) -> p c j i", i=4),
+    )
+
+
+def tile_rows_glin_relu_res_kernel(tc, x, w, r, out):
+    nc = tc.nc
+    with ExitStack() as ctx:
+        sb = ctx.enter_context(tc.tile_pool(name="sb", bufs=1))
+        ps = ctx.enter_context(tc.psum_pool(name="ps", bufs=1))
+        ctx.enter_context(tc.manual_schedule())
+
+        w_raw = sb.tile([P, SETS, PACK, M], F32, name="w_raw")
+        nc.sync.dma_start(
+            out=w_raw[:].rearrange("p s j m -> p s (j m)"),
+            in_=w.rearrange("(s c) (p j) m -> (c p) s (j m)", s=SETS, j=PACK),
+        )
+        x_raw = []
+        for s in range(SETS):
+            t = sb.tile([P, PACK, N], F32, name="x_raw%d" % s)
+            nc.sync.dma_start(
+                out=t[:].rearrange("p j n -> p (j n)"),
+                in_=x[s * SIDE : (s + 1) * SIDE].rearrange("c (p j) n -> (c p) (j n)", j=PACK),
+            )
+            x_raw.append(t)
+        res = []
+        for q in range(G // PAIR):
+            t = sb.tile([P, PAIR, N], F32, name="res%d" % q)
+            nc.sync.dma_start(out=t[:], in_=r[q * PAIR : (q + 1) * PAIR].rearrange("g m n -> m g n"))
+            res.append(t)
+
+        w_bf = sb.tile([P, SETS, M, PACK], BF16, name="w_bf", align_bytes=64)
+        w_codes = sb.tile([P, SETS * M], U32, name="w_codes", align_bytes=64)
+        w_scales = sb.tile([P, SETS * M], U8, name="w_scales", align_bytes=64)
+        for s in range(SETS):
+            interleave(nc.scalar.copy, w_bf[:, s], w_raw[:, s])
+
+        x_codes, x_scales = [], []
+        for s in range(SETS):
+            x_bf = sb.tile([P, N, PACK], BF16, name="x_bf%d" % s, align_bytes=64)
+            codes = sb.tile([P, N], U32, name="x_codes%d" % s, align_bytes=64)
+            scales = sb.tile([P, N], U8, name="x_scales%d" % s, align_bytes=64)
+            interleave(nc.vector.tensor_copy, x_bf[:, :X_SPLIT, :], x_raw[s][:, :, :X_SPLIT])
+            interleave(nc.scalar.copy, x_bf[:, X_SPLIT:, :], x_raw[s][:, :, X_SPLIT:])
+            if s == 0:
+                nc.vector.quantize_mx(
+                    out=w_codes[:].bitcast(FP8X4),
+                    scales=w_scales[:],
+                    in_=w_bf[:].rearrange("p s m j -> p (s m j)"),
+                )
+            nc.vector.quantize_mx(
+                out=codes[:].bitcast(FP8X4),
+                scales=scales[:],
+                in_=x_bf[:].rearrange("p n j -> p (n j)"),
+            )
+            x_codes.append(codes)
+            x_scales.append(scales)
+
+        acc = []
+        for g in range(G):
+            s, c = divmod(g, SIDE)
+            rows = slice(c * ROWS, (c + 1) * ROWS)
+            cols = slice(s * M, (s + 1) * M)
+            bank = ps.tile([M, N], F32, name="acc%d" % g)
+            nc.tensor.matmul_mx(
+                out=bank[:],
+                lhsT=w_codes[rows, cols].bitcast(FP8X4),
+                lhsT_scale=w_scales[rows, cols],
+                rhs=x_codes[s][rows, :].bitcast(FP8X4),
+                rhs_scale=x_scales[s][rows, :],
+                start=True,
+                stop=True,
+            )
+            acc.append(bank)
+
+        for q in range(G // PAIR):
+            y = sb.tile([P, PAIR, N], F32, name="y%d" % q)
+            for e in range(PAIR):
+                nc.vector.scalar_tensor_tensor(
+                    out=y[:, e, :],
+                    in0=acc[q * PAIR + e][:],
+                    scalar=0.0,
+                    in1=res[q][:, e, :],
+                    op0=ALU.max,
+                    op1=ALU.add,
+                )
+            nc.sync.dma_start(out=out[q * PAIR : (q + 1) * PAIR].rearrange("g m n -> m g n"), in_=y[:])

@@ -40,19 +40,26 @@ def tile_rows_glin_relu_res_kernel(tc, x, w, r, out):
             out=w_raw[:].rearrange("p s j m -> p s (j m)"),
             in_=w.rearrange("(s c) (p j) m -> (c p) s (j m)", s=SETS, j=PACK),
         )
-        x_raw = []
-        for s in range(SETS):
+        x_raw, res = [], []
+
+        def load_x(s):
             t = sb.tile([P, PACK, N], F32, name="x_raw%d" % s)
             nc.sync.dma_start(
                 out=t[:].rearrange("p j n -> p (j n)"),
                 in_=x[s * SIDE : (s + 1) * SIDE].rearrange("c (p j) n -> (c p) (j n)", j=PACK),
             )
             x_raw.append(t)
-        res = []
-        for q in range(G // PAIR):
+
+        def load_r(q):
             t = sb.tile([P, PAIR, N], F32, name="res%d" % q)
             nc.sync.dma_start(out=t[:], in_=r[q * PAIR : (q + 1) * PAIR].rearrange("g m n -> m g n"))
             res.append(t)
+
+        load_x(0)
+        load_r(0)
+        load_x(1)
+        for q in range(1, G // PAIR):
+            load_r(q)
 
         w_bf = sb.tile([P, SETS, M, PACK], BF16, name="w_bf", align_bytes=64)
         w_codes = sb.tile([P, SETS * M], U32, name="w_codes", align_bytes=64)
@@ -60,45 +67,38 @@ def tile_rows_glin_relu_res_kernel(tc, x, w, r, out):
         for s in range(SETS):
             interleave(nc.scalar.copy, w_bf[:, s], w_raw[:, s])
 
-        x_codes, x_scales = [], []
-        for s in range(SETS):
+        acc = []
+
+        def round_x(s):
             x_bf = sb.tile([P, N, PACK], BF16, name="x_bf%d" % s, align_bytes=64)
-            codes = sb.tile([P, N], U32, name="x_codes%d" % s, align_bytes=64)
-            scales = sb.tile([P, N], U8, name="x_scales%d" % s, align_bytes=64)
             interleave(nc.vector.tensor_copy, x_bf[:, :X_SPLIT, :], x_raw[s][:, :, :X_SPLIT])
             interleave(nc.scalar.copy, x_bf[:, X_SPLIT:, :], x_raw[s][:, :, X_SPLIT:])
-            if s == 0:
-                nc.vector.quantize_mx(
-                    out=w_codes[:].bitcast(FP8X4),
-                    scales=w_scales[:],
-                    in_=w_bf[:].rearrange("p s m j -> p (s m j)"),
-                )
+            return x_bf
+
+        def multiply(s, x_bf):
+            codes = sb.tile([P, N], U32, name="x_codes%d" % s, align_bytes=64)
+            scales = sb.tile([P, N], U8, name="x_scales%d" % s, align_bytes=64)
             nc.vector.quantize_mx(
                 out=codes[:].bitcast(FP8X4),
                 scales=scales[:],
                 in_=x_bf[:].rearrange("p n j -> p (n j)"),
             )
-            x_codes.append(codes)
-            x_scales.append(scales)
-
-        acc = []
-        for g in range(G):
-            s, c = divmod(g, SIDE)
-            rows = slice(c * ROWS, (c + 1) * ROWS)
             cols = slice(s * M, (s + 1) * M)
-            bank = ps.tile([M, N], F32, name="acc%d" % g)
-            nc.tensor.matmul_mx(
-                out=bank[:],
-                lhsT=w_codes[rows, cols].bitcast(FP8X4),
-                lhsT_scale=w_scales[rows, cols],
-                rhs=x_codes[s][rows, :].bitcast(FP8X4),
-                rhs_scale=x_scales[s][rows, :],
-                start=True,
-                stop=True,
-            )
-            acc.append(bank)
+            for c in range(SIDE):
+                rows = slice(c * ROWS, (c + 1) * ROWS)
+                bank = ps.tile([M, N], F32, name="acc%d" % (s * SIDE + c))
+                nc.tensor.matmul_mx(
+                    out=bank[:],
+                    lhsT=w_codes[rows, cols].bitcast(FP8X4),
+                    lhsT_scale=w_scales[rows, cols],
+                    rhs=codes[rows, :].bitcast(FP8X4),
+                    rhs_scale=scales[rows, :],
+                    start=True,
+                    stop=True,
+                )
+                acc.append(bank)
 
-        for q in range(G // PAIR):
+        def finish(q):
             y = sb.tile([P, PAIR, N], F32, name="y%d" % q)
             for e in range(PAIR):
                 nc.vector.scalar_tensor_tensor(
@@ -110,3 +110,15 @@ def tile_rows_glin_relu_res_kernel(tc, x, w, r, out):
                     op1=ALU.add,
                 )
             nc.sync.dma_start(out=out[q * PAIR : (q + 1) * PAIR].rearrange("g m n -> m g n"), in_=y[:])
+
+        first = round_x(0)
+        nc.vector.quantize_mx(
+            out=w_codes[:].bitcast(FP8X4),
+            scales=w_scales[:],
+            in_=w_bf[:].rearrange("p s m j -> p (s m j)"),
+        )
+        multiply(0, first)
+        finish(0)
+        multiply(1, round_x(1))
+        for q in range(1, G // PAIR):
+            finish(q)

@@ -18,7 +18,8 @@ ROWS = D // PACK
 SIDE = P // ROWS
 SETS = G // SIDE
 PAIR = 2
-X_SPLIT = 352
+HALF = N // 2
+X_SPLIT = 304
 
 
 def interleave(copy, dst, src):
@@ -35,90 +36,87 @@ def tile_rows_glin_relu_res_kernel(tc, x, w, r, out):
         ps = ctx.enter_context(tc.psum_pool(name="ps", bufs=1))
         ctx.enter_context(tc.manual_schedule())
 
-        w_raw = sb.tile([P, SETS, PACK, M], F32, name="w_raw")
-        nc.sync.dma_start(
-            out=w_raw[:].rearrange("p s j m -> p s (j m)"),
-            in_=w.rearrange("(s c) (p j) m -> (c p) s (j m)", s=SETS, j=PACK),
-        )
-        x_raw, res = [], []
-
-        def load_x(s):
-            t = sb.tile([P, PACK, N], F32, name="x_raw%d" % s)
+        def load_set(src, s, name):
+            width = src.shape[2]
+            t = sb.tile([P, PACK, width], F32, name="%s_raw%d" % (name, s))
             nc.sync.dma_start(
                 out=t[:].rearrange("p j n -> p (j n)"),
-                in_=x[s * SIDE : (s + 1) * SIDE].rearrange("c (p j) n -> (c p) (j n)", j=PACK),
+                in_=src[s * SIDE : (s + 1) * SIDE].rearrange("c (p j) n -> (c p) (j n)", j=PACK),
             )
-            x_raw.append(t)
+            return t
 
         def load_r(q):
             t = sb.tile([P, PAIR, N], F32, name="res%d" % q)
             nc.sync.dma_start(out=t[:], in_=r[q * PAIR : (q + 1) * PAIR].rearrange("g m n -> m g n"))
-            res.append(t)
+            return t
 
-        load_x(0)
-        load_r(0)
-        load_x(1)
+        x_raw = [load_set(x, 0, "x")]
+        w_raw = [load_set(w, 0, "w")]
+        x_raw.append(load_set(x, 1, "x"))
+        res = [load_r(0)]
+        w_raw.append(load_set(w, 1, "w"))
         for q in range(1, G // PAIR):
-            load_r(q)
+            res.append(load_r(q))
 
-        w_bf = sb.tile([P, SETS, M, PACK], BF16, name="w_bf", align_bytes=64)
-        w_codes = sb.tile([P, SETS * M], U32, name="w_codes", align_bytes=64)
-        w_scales = sb.tile([P, SETS * M], U8, name="w_scales", align_bytes=64)
-        for s in range(SETS):
-            interleave(nc.scalar.copy, w_bf[:, s], w_raw[:, s])
+        def quantize(codes, scales, values):
+            nc.vector.quantize_mx(
+                out=codes.bitcast(FP8X4), scales=scales, in_=values.rearrange("p n j -> p (n j)")
+            )
+
+        def prepare_x(s):
+            lo = sb.tile([P, HALF, PACK], BF16, name="x_lo%d" % s, align_bytes=64)
+            hi = sb.tile([P, HALF, PACK], BF16, name="x_hi%d" % s, align_bytes=64)
+            codes = sb.tile([P, N], U32, name="x_codes%d" % s, align_bytes=64)
+            scales = sb.tile([P, N], U8, name="x_scales%d" % s, align_bytes=64)
+            interleave(nc.vector.tensor_copy, lo[:], x_raw[s][:, :, :HALF])
+            interleave(nc.vector.tensor_copy, hi[:, : X_SPLIT - HALF, :], x_raw[s][:, :, HALF:X_SPLIT])
+            interleave(nc.scalar.copy, hi[:, X_SPLIT - HALF :, :], x_raw[s][:, :, X_SPLIT:])
+            quantize(codes[:, :HALF], scales[:, :HALF], lo[:])
+            quantize(codes[:, HALF:], scales[:, HALF:], hi[:])
+            return codes, scales
+
+        def prepare_w(s):
+            values = sb.tile([P, M, PACK], BF16, name="w_bf%d" % s, align_bytes=64)
+            codes = sb.tile([P, M], U32, name="w_codes%d" % s, align_bytes=64)
+            scales = sb.tile([P, M], U8, name="w_scales%d" % s, align_bytes=64)
+            interleave(nc.scalar.copy, values[:], w_raw[s][:])
+            quantize(codes[:], scales[:], values[:])
+            return codes, scales
 
         acc = []
 
-        def round_x(s):
-            x_bf = sb.tile([P, N, PACK], BF16, name="x_bf%d" % s, align_bytes=64)
-            interleave(nc.vector.tensor_copy, x_bf[:, :X_SPLIT, :], x_raw[s][:, :, :X_SPLIT])
-            interleave(nc.scalar.copy, x_bf[:, X_SPLIT:, :], x_raw[s][:, :, X_SPLIT:])
-            return x_bf
-
-        def multiply(s, x_bf):
-            codes = sb.tile([P, N], U32, name="x_codes%d" % s, align_bytes=64)
-            scales = sb.tile([P, N], U8, name="x_scales%d" % s, align_bytes=64)
-            nc.vector.quantize_mx(
-                out=codes[:].bitcast(FP8X4),
-                scales=scales[:],
-                in_=x_bf[:].rearrange("p n j -> p (n j)"),
-            )
-            cols = slice(s * M, (s + 1) * M)
+        def multiply(s, wq, xq):
             for c in range(SIDE):
                 rows = slice(c * ROWS, (c + 1) * ROWS)
                 bank = ps.tile([M, N], F32, name="acc%d" % (s * SIDE + c))
                 nc.tensor.matmul_mx(
                     out=bank[:],
-                    lhsT=w_codes[rows, cols].bitcast(FP8X4),
-                    lhsT_scale=w_scales[rows, cols],
-                    rhs=codes[rows, :].bitcast(FP8X4),
-                    rhs_scale=scales[rows, :],
+                    lhsT=wq[0][rows, :].bitcast(FP8X4),
+                    lhsT_scale=wq[1][rows, :],
+                    rhs=xq[0][rows, :].bitcast(FP8X4),
+                    rhs_scale=xq[1][rows, :],
                     start=True,
                     stop=True,
                 )
                 acc.append(bank)
 
-        def finish(q):
-            y = sb.tile([P, PAIR, N], F32, name="y%d" % q)
-            for e in range(PAIR):
-                nc.vector.scalar_tensor_tensor(
-                    out=y[:, e, :],
-                    in0=acc[q * PAIR + e][:],
-                    scalar=0.0,
-                    in1=res[q][:, e, :],
-                    op0=ALU.max,
-                    op1=ALU.add,
-                )
-            nc.sync.dma_start(out=out[q * PAIR : (q + 1) * PAIR].rearrange("g m n -> m g n"), in_=y[:])
+        def finish(g):
+            y = sb.tile([P, N], F32, name="y%d" % g)
+            nc.vector.scalar_tensor_tensor(
+                out=y[:],
+                in0=acc[g][:],
+                scalar=0.0,
+                in1=res[g // PAIR][:, g % PAIR, :],
+                op0=ALU.max,
+                op1=ALU.add,
+            )
+            nc.sync.dma_start(out=out[g], in_=y[:])
 
-        first = round_x(0)
-        nc.vector.quantize_mx(
-            out=w_codes[:].bitcast(FP8X4),
-            scales=w_scales[:],
-            in_=w_bf[:].rearrange("p s m j -> p (s m j)"),
-        )
-        multiply(0, first)
+        xq = prepare_x(0)
+        multiply(0, prepare_w(0), xq)
+        xq = prepare_x(1)
         finish(0)
-        multiply(1, round_x(1))
-        for q in range(1, G // PAIR):
-            finish(q)
+        finish(1)
+        multiply(1, prepare_w(1), xq)
+        for g in range(2, G):
+            finish(g)

@@ -17,9 +17,9 @@ PACK = 4
 ROWS = D // PACK
 SIDE = P // ROWS
 SETS = G // SIDE
-PAIR = 2
 HALF = N // 2
 X_SPLIT = 304
+SHARED = SIDE - 1
 
 
 def interleave(copy, dst, src):
@@ -45,23 +45,38 @@ def tile_rows_glin_relu_res_kernel(tc, x, w, r, out):
             )
             return t
 
-        def load_r(q):
-            t = sb.tile([P, PAIR, N], F32, name="res%d" % q)
-            nc.sync.dma_start(out=t[:], in_=r[q * PAIR : (q + 1) * PAIR].rearrange("g m n -> m g n"))
+        def paired(t, c):
+            return t.rearrange("(s c) (q i) n -> c q s (i n)", s=SETS, i=SETS)[c]
+
+        def load_r(c):
+            t = sb.tile([P, SETS * N], F32, name="res%d" % c)
+            nc.sync.dma_start(out=t[:], in_=paired(r, c))
+            return t
+
+        def load_r_alone(g):
+            t = sb.tile([P, N], F32, name="res_alone%d" % g)
+            nc.sync.dma_start(out=t[:], in_=r[g])
             return t
 
         x_raw = [load_set(x, 0, "x")]
-        w_raw = [load_set(w, 0, "w")]
+        w_raw = sb.tile([P, SETS, PACK, M], F32, name="w_raw")
+        nc.sync.dma_start(
+            out=w_raw[:].rearrange("p s j m -> p s (j m)"),
+            in_=w.rearrange("(s c) (p j) m -> (c p) s (j m)", s=SETS, j=PACK),
+        )
         x_raw.append(load_set(x, 1, "x"))
-        res = [load_r(0)]
-        w_raw.append(load_set(w, 1, "w"))
-        for q in range(1, G // PAIR):
-            res.append(load_r(q))
+        res_alone = [load_r_alone(SHARED)]
+        res = [load_r(c) for c in range(SHARED)]
+        res_alone.append(load_r_alone(SIDE + SHARED))
+
+        w_bf = []
+        for s in range(SETS):
+            t = sb.tile([P, SETS, M // SETS, SETS, PACK], BF16, name="w_bf%d" % s, align_bytes=64)
+            nc.vector.memset(t[:], 0.0)
+            w_bf.append(t)
 
         def quantize(codes, scales, values):
-            nc.vector.quantize_mx(
-                out=codes.bitcast(FP8X4), scales=scales, in_=values.rearrange("p n j -> p (n j)")
-            )
+            nc.vector.quantize_mx(out=codes.bitcast(FP8X4), scales=scales, in_=values)
 
         def prepare_x(s):
             lo = sb.tile([P, HALF, PACK], BF16, name="x_lo%d" % s, align_bytes=64)
@@ -71,52 +86,68 @@ def tile_rows_glin_relu_res_kernel(tc, x, w, r, out):
             interleave(nc.vector.tensor_copy, lo[:], x_raw[s][:, :, :HALF])
             interleave(nc.vector.tensor_copy, hi[:, : X_SPLIT - HALF, :], x_raw[s][:, :, HALF:X_SPLIT])
             interleave(nc.scalar.copy, hi[:, X_SPLIT - HALF :, :], x_raw[s][:, :, X_SPLIT:])
-            quantize(codes[:, :HALF], scales[:, :HALF], lo[:])
-            quantize(codes[:, HALF:], scales[:, HALF:], hi[:])
+            quantize(codes[:, :HALF], scales[:, :HALF], lo[:].rearrange("p n j -> p (n j)"))
+            quantize(codes[:, HALF:], scales[:, HALF:], hi[:].rearrange("p n j -> p (n j)"))
             return codes, scales
 
         def prepare_w(s):
-            values = sb.tile([P, M, PACK], BF16, name="w_bf%d" % s, align_bytes=64)
-            codes = sb.tile([P, M], U32, name="w_codes%d" % s, align_bytes=64)
-            scales = sb.tile([P, M], U8, name="w_scales%d" % s, align_bytes=64)
-            interleave(nc.scalar.copy, values[:], w_raw[s][:])
-            quantize(codes[:], scales[:], values[:])
+            codes = sb.tile([P, SETS * M], U32, name="w_codes%d" % s, align_bytes=64)
+            scales = sb.tile([P, SETS * M], U8, name="w_scales%d" % s, align_bytes=64)
+            nc.scalar.copy(
+                out=w_bf[s][: SHARED * ROWS, :, :, s, :],
+                in_=w_raw[: SHARED * ROWS, s].rearrange("p j (q i) -> p i q j", i=SETS),
+            )
+            interleave(
+                nc.vector.tensor_copy,
+                w_bf[s][SHARED * ROWS :, 0].rearrange("p q t j -> p (q t) j"),
+                w_raw[SHARED * ROWS :, s],
+            )
+            quantize(codes[:], scales[:], w_bf[s][:].rearrange("p i q t j -> p (i q t j)"))
             return codes, scales
 
-        acc = []
+        acc = [[ps.tile([M, N], F32, name="acc%d_%d" % (c, i)) for i in range(SETS)] for c in range(SIDE)]
 
-        def multiply(s, wq, xq):
-            for c in range(SIDE):
-                rows = slice(c * ROWS, (c + 1) * ROWS)
-                bank = ps.tile([M, N], F32, name="acc%d" % (s * SIDE + c))
-                nc.tensor.matmul_mx(
-                    out=bank[:],
-                    lhsT=wq[0][rows, :].bitcast(FP8X4),
-                    lhsT_scale=wq[1][rows, :],
-                    rhs=xq[0][rows, :].bitcast(FP8X4),
-                    rhs_scale=xq[1][rows, :],
-                    start=True,
-                    stop=True,
-                )
-                acc.append(bank)
-
-        def finish(g):
-            y = sb.tile([P, N], F32, name="y%d" % g)
-            nc.vector.scalar_tensor_tensor(
-                out=y[:],
-                in0=acc[g][:],
-                scalar=0.0,
-                in1=res[g // PAIR][:, g % PAIR, :],
-                op0=ALU.max,
-                op1=ALU.add,
+        def multiply(bank, c, i, wq, xq, start, stop):
+            rows = slice(c * ROWS, (c + 1) * ROWS)
+            cols = slice(i * M, (i + 1) * M)
+            nc.tensor.matmul_mx(
+                out=bank[:],
+                lhsT=wq[0][rows, cols].bitcast(FP8X4),
+                lhsT_scale=wq[1][rows, cols],
+                rhs=xq[0][rows, :].bitcast(FP8X4),
+                rhs_scale=xq[1][rows, :],
+                start=start,
+                stop=stop,
             )
-            nc.sync.dma_start(out=out[g], in_=y[:])
+
+        def multiply_set(s, wq, xq):
+            multiply(acc[SHARED][s], SHARED, 0, wq, xq, True, True)
+            for i in range(SETS):
+                for c in range(SHARED):
+                    multiply(acc[c][i], c, i, wq, xq, s == 0, s == SETS - 1)
+
+        def relu_add(y, bank, residual):
+            nc.vector.scalar_tensor_tensor(
+                out=y, in0=bank[:], scalar=0.0, in1=residual, op0=ALU.max, op1=ALU.add
+            )
+
+        def finish(c):
+            y = sb.tile([P, SETS * N], F32, name="y%d" % c)
+            for i in range(SETS):
+                cols = slice(i * N, (i + 1) * N)
+                relu_add(y[:, cols], acc[c][i], res[c][:, cols])
+            nc.sync.dma_start(out=paired(out, c), in_=y[:])
+
+        def finish_alone(s):
+            y = sb.tile([P, N], F32, name="y_alone%d" % s)
+            relu_add(y[:], acc[SHARED][s], res_alone[s][:])
+            nc.sync.dma_start(out=out[s * SIDE + SHARED], in_=y[:])
 
         xq = prepare_x(0)
-        multiply(0, prepare_w(0), xq)
-        xq = prepare_x(1)
-        finish(0)
-        finish(1)
-        multiply(1, prepare_w(1), xq)
-        for g in range(2, G):
-            finish(g)
+        wq = [prepare_w(s) for s in range(SETS)]
+        multiply_set(0, wq[0], xq)
+        multiply_set(1, wq[1], prepare_x(1))
+        finish_alone(0)
+        for c in range(SHARED):
+            finish(c)
+        finish_alone(1)

@@ -58,16 +58,14 @@ def tile_rows_glin_relu_res_kernel(tc, x, w, r, out):
             nc.sync.dma_start(out=t[:], in_=r[g])
             return t
 
-        x_raw = [load_set(x, 0, "x")]
         w_raw = sb.tile([P, SETS, PACK, M], F32, name="w_raw")
         nc.sync.dma_start(
             out=w_raw[:].rearrange("p s j m -> p s (j m)"),
             in_=w.rearrange("(s c) (p j) m -> (c p) s (j m)", s=SETS, j=PACK),
         )
-        x_raw.append(load_set(x, 1, "x"))
-        res_alone = [load_r_alone(SHARED)]
+        x_raw = [load_set(x, s, "x") for s in range(SETS)]
+        res_alone = [load_r_alone(s * SIDE + SHARED) for s in range(SETS)]
         res = [load_r(c) for c in range(SHARED)]
-        res_alone.append(load_r_alone(SIDE + SHARED))
 
         w_bf = []
         for s in range(SETS):
@@ -93,12 +91,12 @@ def tile_rows_glin_relu_res_kernel(tc, x, w, r, out):
         def prepare_w(s):
             codes = sb.tile([P, SETS * M], U32, name="w_codes%d" % s, align_bytes=64)
             scales = sb.tile([P, SETS * M], U8, name="w_scales%d" % s, align_bytes=64)
-            nc.scalar.copy(
+            nc.vector.tensor_copy(
                 out=w_bf[s][: SHARED * ROWS, :, :, s, :],
                 in_=w_raw[: SHARED * ROWS, s].rearrange("p j (q i) -> p i q j", i=SETS),
             )
             interleave(
-                nc.vector.tensor_copy,
+                nc.scalar.copy,
                 w_bf[s][SHARED * ROWS :, 0].rearrange("p q t j -> p (q t) j"),
                 w_raw[SHARED * ROWS :, s],
             )
@@ -143,11 +141,10 @@ def tile_rows_glin_relu_res_kernel(tc, x, w, r, out):
             relu_add(y[:], acc[SHARED][s], res_alone[s][:])
             nc.sync.dma_start(out=out[s * SIDE + SHARED], in_=y[:])
 
-        xq = prepare_x(0)
         wq = [prepare_w(s) for s in range(SETS)]
-        multiply_set(0, wq[0], xq)
-        multiply_set(1, wq[1], prepare_x(1))
-        finish_alone(0)
+        for s in range(SETS):
+            multiply_set(s, wq[s], prepare_x(s))
+        for s in range(SETS):
+            finish_alone(s)
         for c in range(SHARED):
             finish(c)
-        finish_alone(1)

@@ -70,8 +70,15 @@ def tile_rows_glin_relu_res_kernel(tc, x, w, r, out):
         w_bf = []
         for s in range(SETS):
             t = sb.tile([P, SETS, M // SETS, SETS, PACK], BF16, name="w_bf%d" % s, align_bytes=64)
-            nc.vector.memset(t[:], 0.0)
             w_bf.append(t)
+        nc.vector.memset(w_bf[0][: SHARED * ROWS], 0.0)
+        nc.vector.memset(w_bf[1][:], 0.0)
+        nc.scalar.copy(
+            out=w_bf[0][SHARED * ROWS :].rearrange("p s q t j -> p s (q t j)").rearrange(
+                "p s (c i j) -> p s c j i", i=4, j=PACK
+            ),
+            in_=w_raw[SHARED * ROWS :].rearrange("p s j (c i) -> p s c j i", i=4),
+        )
 
         def quantize(codes, scales, values):
             nc.vector.quantize_mx(out=codes.bitcast(FP8X4), scales=scales, in_=values)
@@ -95,11 +102,6 @@ def tile_rows_glin_relu_res_kernel(tc, x, w, r, out):
                 out=w_bf[s][: SHARED * ROWS, :, :, s, :],
                 in_=w_raw[: SHARED * ROWS, s].rearrange("p j (q i) -> p i q j", i=SETS),
             )
-            interleave(
-                nc.scalar.copy,
-                w_bf[s][SHARED * ROWS :, 0].rearrange("p q t j -> p (q t) j"),
-                w_raw[SHARED * ROWS :, s],
-            )
             quantize(codes[:], scales[:], w_bf[s][:].rearrange("p i q t j -> p (i q t j)"))
             return codes, scales
 
@@ -118,11 +120,11 @@ def tile_rows_glin_relu_res_kernel(tc, x, w, r, out):
                 stop=stop,
             )
 
-        def multiply_set(s, wq, xq):
-            multiply(acc[SHARED][s], SHARED, 0, wq, xq, True, True)
+        def multiply_set(s, xq):
+            multiply(acc[SHARED][s], SHARED, s, wq[0], xq, True, True)
             for i in range(SETS):
                 for c in range(SHARED):
-                    multiply(acc[c][i], c, i, wq, xq, s == 0, s == SETS - 1)
+                    multiply(acc[c][i], c, i, wq[s], xq, s == 0, s == SETS - 1)
 
         def relu_add(y, bank, residual):
             nc.vector.scalar_tensor_tensor(
@@ -141,9 +143,9 @@ def tile_rows_glin_relu_res_kernel(tc, x, w, r, out):
             relu_add(y[:], acc[SHARED][s], res_alone[s][:])
             nc.sync.dma_start(out=out[s * SIDE + SHARED], in_=y[:])
 
-        wq = [prepare_w(s) for s in range(SETS)]
+        wq = {s: prepare_w(s) for s in reversed(range(SETS))}
         for s in range(SETS):
-            multiply_set(s, wq[s], prepare_x(s))
+            multiply_set(s, prepare_x(s))
         for s in range(SETS):
             finish_alone(s)
         for c in range(SHARED):

@@ -11,6 +11,7 @@ U32 = mybir.dt.uint32
 U8 = mybir.dt.uint8
 FP8X4 = mybir.dt.float8_e4m3fn_x4
 ALU = mybir.AluOpType
+ACT = mybir.ActivationFunctionType
 
 P = 128
 PACK = 4
@@ -64,8 +65,10 @@ def tile_rows_glin_relu_res_kernel(tc, x, w, r, out):
             in_=w.rearrange("(s c) (p j) m -> (c p) s (j m)", s=SETS, j=PACK),
         )
         x_raw = [load_set(x, s, "x") for s in range(SETS)]
-        res_alone = [load_r_alone(s * SIDE + SHARED) for s in range(SETS)]
-        res = [load_r(c) for c in range(SHARED)]
+        res_alone = [load_r_alone(SHARED)]
+        res = [load_r(0)]
+        res_alone.append(load_r_alone(SIDE + SHARED))
+        res.extend(load_r(c) for c in range(1, SHARED))
 
         w_bf = []
         for s in range(SETS):
@@ -138,15 +141,30 @@ def tile_rows_glin_relu_res_kernel(tc, x, w, r, out):
                 relu_add(y[:, cols], acc[c][i], res[c][:, cols])
             nc.sync.dma_start(out=paired(out, c), in_=y[:])
 
+        def finish_by_bank(c):
+            for i in range(SETS):
+                cols = slice(i * N, (i + 1) * N)
+                y = sb.tile([P, N], F32, name="y%d_%d" % (c, i))
+                relu_add(y[:], acc[c][i], res[c][:, cols])
+                nc.sync.dma_start(out=paired(out, c)[:, :, cols], in_=y[:])
+
         def finish_alone(s):
             y = sb.tile([P, N], F32, name="y_alone%d" % s)
             relu_add(y[:], acc[SHARED][s], res_alone[s][:])
             nc.sync.dma_start(out=out[s * SIDE + SHARED], in_=y[:])
 
+        def finish_alone_off_vector(s):
+            z = sb.tile([P, N], F32, name="z_alone%d" % s)
+            y = sb.tile([P, N], F32, name="y_alone%d" % s)
+            nc.scalar.activation(out=z[:], in_=acc[SHARED][s][:], func=ACT.Relu)
+            nc.gpsimd.tensor_tensor(out=y[:], in0=z[:], in1=res_alone[s][:], op=ALU.add)
+            nc.sync.dma_start(out=out[s * SIDE + SHARED], in_=y[:])
+
         wq = {s: prepare_w(s) for s in reversed(range(SETS))}
         for s in range(SETS):
             multiply_set(s, prepare_x(s))
-        for s in range(SETS):
-            finish_alone(s)
-        for c in range(SHARED):
+        finish_alone(0)
+        finish_by_bank(0)
+        finish_alone_off_vector(1)
+        for c in range(1, SHARED):
             finish(c)

@@ -39,7 +39,7 @@ def tile_rows_glin_relu_res_kernel(tc, x, w, r, out):
 
         def load_set(src, s, name):
             width = src.shape[2]
-            t = sb.tile([P, PACK, width], F32, name="%s_raw%d" % (name, s))
+            t = sb.tile([P, PACK, width], F32, name="%s_raw%d" % (name, s), align_bytes=256)
             nc.sync.dma_start(
                 out=t[:].rearrange("p j n -> p (j n)"),
                 in_=src[s * SIDE : (s + 1) * SIDE].rearrange("c (p j) n -> (c p) (j n)", j=PACK),
@@ -50,16 +50,16 @@ def tile_rows_glin_relu_res_kernel(tc, x, w, r, out):
             return t.rearrange("(s c) (q i) n -> c q s (i n)", s=SETS, i=SETS)[c]
 
         def load_r(c):
-            t = sb.tile([P, SETS * N], F32, name="res%d" % c)
+            t = sb.tile([P, SETS * N], F32, name="res%d" % c, align_bytes=256)
             nc.sync.dma_start(out=t[:], in_=paired(r, c))
             return t
 
         def load_r_alone(g):
-            t = sb.tile([P, N], F32, name="res_alone%d" % g)
+            t = sb.tile([P, N], F32, name="res_alone%d" % g, align_bytes=256)
             nc.sync.dma_start(out=t[:], in_=r[g])
             return t
 
-        w_raw = sb.tile([P, SETS, PACK, M], F32, name="w_raw")
+        w_raw = sb.tile([P, SETS, PACK, M], F32, name="w_raw", align_bytes=256)
         nc.sync.dma_start(
             out=w_raw[:].rearrange("p s j m -> p s (j m)"),
             in_=w.rearrange("(s c) (p j) m -> (c p) s (j m)", s=SETS, j=PACK),
@@ -135,7 +135,7 @@ def tile_rows_glin_relu_res_kernel(tc, x, w, r, out):
             )
 
         def finish(c):
-            y = sb.tile([P, SETS * N], F32, name="y%d" % c)
+            y = sb.tile([P, SETS * N], F32, name="y%d" % c, align_bytes=256)
             for i in range(SETS):
                 cols = slice(i * N, (i + 1) * N)
                 relu_add(y[:, cols], acc[c][i], res[c][:, cols])
@@ -144,18 +144,18 @@ def tile_rows_glin_relu_res_kernel(tc, x, w, r, out):
         def finish_by_bank(c):
             for i in range(SETS):
                 cols = slice(i * N, (i + 1) * N)
-                y = sb.tile([P, N], F32, name="y%d_%d" % (c, i))
+                y = sb.tile([P, N], F32, name="y%d_%d" % (c, i), align_bytes=256)
                 relu_add(y[:], acc[c][i], res[c][:, cols])
                 nc.sync.dma_start(out=paired(out, c)[:, :, cols], in_=y[:])
 
         def finish_alone(s):
-            y = sb.tile([P, N], F32, name="y_alone%d" % s)
+            y = sb.tile([P, N], F32, name="y_alone%d" % s, align_bytes=256)
             relu_add(y[:], acc[SHARED][s], res_alone[s][:])
             nc.sync.dma_start(out=out[s * SIDE + SHARED], in_=y[:])
 
         def finish_alone_off_vector(s):
-            z = sb.tile([P, N], F32, name="z_alone%d" % s)
-            y = sb.tile([P, N], F32, name="y_alone%d" % s)
+            z = sb.tile([P, N], F32, name="z_alone%d" % s, align_bytes=256)
+            y = sb.tile([P, N], F32, name="y_alone%d" % s, align_bytes=256)
             nc.scalar.activation(out=z[:], in_=acc[SHARED][s][:], func=ACT.Relu)
             nc.gpsimd.tensor_tensor(out=y[:], in0=z[:], in1=res_alone[s][:], op=ALU.add)
             nc.sync.dma_start(out=out[s * SIDE + SHARED], in_=y[:])

@@ -86,25 +86,30 @@ def tile_rows_glin_relu_res_kernel(tc, x, w, r, out):
         def quantize(codes, scales, values):
             nc.vector.quantize_mx(out=codes.bitcast(FP8X4), scales=scales, in_=values)
 
-        def prepare_x(s):
+        def round_x(s):
             lo = sb.tile([P, HALF, PACK], BF16, name="x_lo%d" % s, align_bytes=64)
             hi = sb.tile([P, HALF, PACK], BF16, name="x_hi%d" % s, align_bytes=64)
-            codes = sb.tile([P, N], U32, name="x_codes%d" % s, align_bytes=64)
-            scales = sb.tile([P, N], U8, name="x_scales%d" % s, align_bytes=64)
             interleave(nc.vector.tensor_copy, lo[:], x_raw[s][:, :, :HALF])
             interleave(nc.vector.tensor_copy, hi[:, : X_SPLIT - HALF, :], x_raw[s][:, :, HALF:X_SPLIT])
             interleave(nc.scalar.copy, hi[:, X_SPLIT - HALF :, :], x_raw[s][:, :, X_SPLIT:])
+            return lo, hi
+
+        def quantize_x(s, lo, hi):
+            codes = sb.tile([P, N], U32, name="x_codes%d" % s, align_bytes=64)
+            scales = sb.tile([P, N], U8, name="x_scales%d" % s, align_bytes=64)
             quantize(codes[:, :HALF], scales[:, :HALF], lo[:].rearrange("p n j -> p (n j)"))
             quantize(codes[:, HALF:], scales[:, HALF:], hi[:].rearrange("p n j -> p (n j)"))
             return codes, scales
 
-        def prepare_w(s):
-            codes = sb.tile([P, SETS * M], U32, name="w_codes%d" % s, align_bytes=64)
-            scales = sb.tile([P, SETS * M], U8, name="w_scales%d" % s, align_bytes=64)
-            nc.vector.tensor_copy(
+        def round_w(s, copy):
+            copy(
                 out=w_bf[s][: SHARED * ROWS, :, :, s, :],
                 in_=w_raw[: SHARED * ROWS, s].rearrange("p j (q i) -> p i q j", i=SETS),
             )
+
+        def quantize_w(s):
+            codes = sb.tile([P, SETS * M], U32, name="w_codes%d" % s, align_bytes=64)
+            scales = sb.tile([P, SETS * M], U8, name="w_scales%d" % s, align_bytes=64)
             quantize(codes[:], scales[:], w_bf[s][:].rearrange("p i q t j -> p (i q t j)"))
             return codes, scales
 
@@ -124,10 +129,11 @@ def tile_rows_glin_relu_res_kernel(tc, x, w, r, out):
             )
 
         def multiply_set(s, xq):
-            multiply(acc[SHARED][s], SHARED, s, wq[0], xq, True, True)
             for i in range(SETS):
                 for c in range(SHARED):
                     multiply(acc[c][i], c, i, wq[s], xq, s == 0, s == SETS - 1)
+                    if i == 0 and c == 0:
+                        multiply(acc[SHARED][s], SHARED, s, wq[0], xq, True, True)
 
         def relu_add(y, bank, residual):
             nc.vector.scalar_tensor_tensor(
@@ -154,15 +160,21 @@ def tile_rows_glin_relu_res_kernel(tc, x, w, r, out):
             nc.sync.dma_start(out=out[s * SIDE + SHARED], in_=y[:])
 
         def finish_alone_off_vector(s):
-            z = sb.tile([P, N], F32, name="z_alone%d" % s, align_bytes=256)
             y = sb.tile([P, N], F32, name="y_alone%d" % s, align_bytes=256)
-            nc.scalar.activation(out=z[:], in_=acc[SHARED][s][:], func=ACT.Relu)
-            nc.gpsimd.tensor_tensor(out=y[:], in0=z[:], in1=res_alone[s][:], op=ALU.add)
+            for h in range(N // HALF):
+                cols = slice(h * HALF, (h + 1) * HALF)
+                z = sb.tile([P, HALF], F32, name="z_alone%d_%d" % (s, h), align_bytes=256)
+                nc.scalar.activation(out=z[:], in_=acc[SHARED][s][:, cols], func=ACT.Relu)
+                nc.gpsimd.tensor_tensor(out=y[:, cols], in0=z[:], in1=res_alone[s][:, cols], op=ALU.add)
             nc.sync.dma_start(out=out[s * SIDE + SHARED], in_=y[:])
 
-        wq = {s: prepare_w(s) for s in reversed(range(SETS))}
-        for s in range(SETS):
-            multiply_set(s, prepare_x(s))
+        round_w(0, nc.scalar.copy)
+        round_w(1, nc.vector.tensor_copy)
+        wq = {1: quantize_w(1)}
+        x_bf = round_x(0)
+        wq[0] = quantize_w(0)
+        multiply_set(0, quantize_x(0, *x_bf))
+        multiply_set(1, quantize_x(1, *round_x(1)))
         finish_alone(0)
         finish_by_bank(0)
         finish_alone_off_vector(1)

@@ -20,7 +20,7 @@ SIDE = P // ROWS
 SETS = G // SIDE
 HALF = N // 2
 X_SPLIT = 304
-SHARED = SIDE - 1
+SHARED = SIDE // 2
 
 
 def interleave(copy, dst, src):
@@ -65,10 +65,13 @@ def tile_rows_glin_relu_res_kernel(tc, x, w, r, out):
             in_=w.rearrange("(s c) (p j) m -> (c p) s (j m)", s=SETS, j=PACK),
         )
         x_raw = [load_set(x, s, "x") for s in range(SETS)]
-        res_alone = [load_r_alone(SHARED)]
-        res = [load_r(0)]
-        res_alone.append(load_r_alone(SIDE + SHARED))
-        res.extend(load_r(c) for c in range(1, SHARED))
+        res_alone = {}
+        res = []
+        for s in range(SETS):
+            for c in range(SHARED, SIDE):
+                res_alone[s * SIDE + c] = load_r_alone(s * SIDE + c)
+                if s * SIDE + c in (SIDE - 1, G - 1):
+                    res.append(load_r(s))
 
         w_bf = []
         for s in range(SETS):
@@ -129,11 +132,13 @@ def tile_rows_glin_relu_res_kernel(tc, x, w, r, out):
             )
 
         def multiply_set(s, xq):
-            for i in range(SETS):
-                for c in range(SHARED):
-                    multiply(acc[c][i], c, i, wq[s], xq, s == 0, s == SETS - 1)
-                    if i == 0 and c == 0:
-                        multiply(acc[SHARED][s], SHARED, s, wq[0], xq, True, True)
+            for c in range(SIDE):
+                if c < SHARED:
+                    multiply(acc[c][0], c, 0, wq[s], xq, s == 0, s == SETS - 1)
+                else:
+                    multiply(acc[c][s], c, s, wq[0], xq, True, True)
+            for c in range(SHARED):
+                multiply(acc[c][1], c, 1, wq[s], xq, s == 0, s == SETS - 1)
 
         def relu_add(y, bank, residual):
             nc.vector.scalar_tensor_tensor(
@@ -154,19 +159,19 @@ def tile_rows_glin_relu_res_kernel(tc, x, w, r, out):
                 relu_add(y[:], acc[c][i], res[c][:, cols])
                 nc.sync.dma_start(out=paired(out, c)[:, :, cols], in_=y[:])
 
-        def finish_alone(s):
-            y = sb.tile([P, N], F32, name="y_alone%d" % s, align_bytes=256)
-            relu_add(y[:], acc[SHARED][s], res_alone[s][:])
-            nc.sync.dma_start(out=out[s * SIDE + SHARED], in_=y[:])
+        def finish_alone(g):
+            y = sb.tile([P, N], F32, name="y_alone%d" % g, align_bytes=256)
+            relu_add(y[:], acc[g % SIDE][g // SIDE], res_alone[g][:])
+            nc.sync.dma_start(out=out[g], in_=y[:])
 
-        def finish_alone_off_vector(s):
-            y = sb.tile([P, N], F32, name="y_alone%d" % s, align_bytes=256)
+        def finish_alone_off_vector(g):
+            y = sb.tile([P, N], F32, name="y_alone%d" % g, align_bytes=256)
             for h in range(N // HALF):
                 cols = slice(h * HALF, (h + 1) * HALF)
-                z = sb.tile([P, HALF], F32, name="z_alone%d_%d" % (s, h), align_bytes=256)
-                nc.scalar.activation(out=z[:], in_=acc[SHARED][s][:, cols], func=ACT.Relu)
-                nc.gpsimd.tensor_tensor(out=y[:, cols], in0=z[:], in1=res_alone[s][:, cols], op=ALU.add)
-            nc.sync.dma_start(out=out[s * SIDE + SHARED], in_=y[:])
+                z = sb.tile([P, HALF], F32, name="z_alone%d_%d" % (g, h), align_bytes=256)
+                nc.scalar.activation(out=z[:], in_=acc[g % SIDE][g // SIDE][:, cols], func=ACT.Relu)
+                nc.gpsimd.tensor_tensor(out=y[:, cols], in0=z[:], in1=res_alone[g][:, cols], op=ALU.add)
+            nc.sync.dma_start(out=out[g], in_=y[:])
 
         round_w(0, nc.scalar.copy)
         round_w(1, nc.vector.tensor_copy)
@@ -175,8 +180,9 @@ def tile_rows_glin_relu_res_kernel(tc, x, w, r, out):
         wq[0] = quantize_w(0)
         multiply_set(0, quantize_x(0, *x_bf))
         multiply_set(1, quantize_x(1, *round_x(1)))
-        finish_alone(0)
+        finish_alone(2)
+        finish_alone(3)
         finish_by_bank(0)
-        finish_alone_off_vector(1)
-        for c in range(1, SHARED):
-            finish(c)
+        finish_alone_off_vector(6)
+        finish_alone(7)
+        finish(1)

@@ -142,26 +142,29 @@ def tile_rows_glin_relu_res_kernel(tc, x, w, r, out):
 
         def relu_add(y, bank, residual):
             nc.vector.scalar_tensor_tensor(
-                out=y, in0=bank[:], scalar=0.0, in1=residual, op0=ALU.max, op1=ALU.add
+                out=y, in0=bank, scalar=0.0, in1=residual, op0=ALU.max, op1=ALU.add
             )
 
         def finish(c):
             y = sb.tile([P, SETS * N], F32, name="y%d" % c, align_bytes=256)
-            for i in range(SETS):
-                cols = slice(i * N, (i + 1) * N)
-                relu_add(y[:, cols], acc[c][i], res[c][:, cols])
+            z = sb.tile([P, HALF], F32, name="z%d" % c, align_bytes=256)
+            last = slice(N + HALF, SETS * N)
+            nc.scalar.activation(out=z[:], in_=acc[c][1][:, HALF:], func=ACT.Relu)
+            nc.gpsimd.tensor_tensor(out=y[:, last], in0=z[:], in1=res[c][:, last], op=ALU.add)
+            relu_add(y[:, :N], acc[c][0][:], res[c][:, :N])
+            relu_add(y[:, N : N + HALF], acc[c][1][:, :HALF], res[c][:, N : N + HALF])
             nc.sync.dma_start(out=paired(out, c), in_=y[:])
 
         def finish_by_bank(c):
             for i in range(SETS):
                 cols = slice(i * N, (i + 1) * N)
                 y = sb.tile([P, N], F32, name="y%d_%d" % (c, i), align_bytes=256)
-                relu_add(y[:], acc[c][i], res[c][:, cols])
+                relu_add(y[:], acc[c][i][:], res[c][:, cols])
                 nc.sync.dma_start(out=paired(out, c)[:, :, cols], in_=y[:])
 
         def finish_alone(g):
             y = sb.tile([P, N], F32, name="y_alone%d" % g, align_bytes=256)
-            relu_add(y[:], acc[g % SIDE][g // SIDE], res_alone[g][:])
+            relu_add(y[:], acc[g % SIDE][g // SIDE][:], res_alone[g][:])
             nc.sync.dma_start(out=out[g], in_=y[:])
 
         def finish_alone_off_vector(g):

@@ -18,16 +18,24 @@ PACK = 4
 ROWS = D // PACK
 SIDE = P // ROWS
 SETS = G // SIDE
-HALF = N // 2
-X_SPLIT = 304
 SHARED = SIDE // 2
+SHARED_P = SHARED * ROWS
+HALF = N // 2
+RUN = 4
+X_SPLIT = 304
+MX_ALIGN = 64
+DMA_ALIGN = 256
 
 
 def interleave(copy, dst, src):
     copy(
-        out=dst.rearrange("p (c i) j -> p c j i", i=4),
-        in_=src.rearrange("p j (c i) -> p c j i", i=4),
+        out=dst.rearrange("p (a b) j -> p a j b", b=RUN),
+        in_=src.rearrange("p j (a b) -> p a j b", b=RUN),
     )
+
+
+def paired(t, c):
+    return t.rearrange("(s c) (q i) n -> c q s (i n)", s=SETS, i=SETS)[c]
 
 
 def tile_rows_glin_relu_res_kernel(tc, x, w, r, out):
@@ -37,155 +45,164 @@ def tile_rows_glin_relu_res_kernel(tc, x, w, r, out):
         ps = ctx.enter_context(tc.psum_pool(name="ps", bufs=1))
         ctx.enter_context(tc.manual_schedule())
 
-        def load_set(src, s, name):
-            width = src.shape[2]
-            t = sb.tile([P, PACK, width], F32, name="%s_raw%d" % (name, s), align_bytes=256)
+        def load_x(s):
+            t = sb.tile([P, PACK, N], F32, name="x_raw%d" % s, align_bytes=DMA_ALIGN)
             nc.sync.dma_start(
                 out=t[:].rearrange("p j n -> p (j n)"),
-                in_=src[s * SIDE : (s + 1) * SIDE].rearrange("c (p j) n -> (c p) (j n)", j=PACK),
+                in_=x[s * SIDE : (s + 1) * SIDE].rearrange("c (p j) n -> (c p) (j n)", j=PACK),
             )
             return t
 
-        def paired(t, c):
-            return t.rearrange("(s c) (q i) n -> c q s (i n)", s=SETS, i=SETS)[c]
-
-        def load_r(c):
-            t = sb.tile([P, SETS * N], F32, name="res%d" % c, align_bytes=256)
+        def load_r_shared(c):
+            t = sb.tile([P, SETS * N], F32, name="r_shared%d" % c, align_bytes=DMA_ALIGN)
             nc.sync.dma_start(out=t[:], in_=paired(r, c))
             return t
 
-        def load_r_alone(g):
-            t = sb.tile([P, N], F32, name="res_alone%d" % g, align_bytes=256)
+        def load_r_lone(g):
+            t = sb.tile([P, N], F32, name="r_lone%d" % g, align_bytes=DMA_ALIGN)
             nc.sync.dma_start(out=t[:], in_=r[g])
             return t
 
-        w_raw = sb.tile([P, SETS, PACK, M], F32, name="w_raw", align_bytes=256)
+        w_raw = sb.tile([P, SETS, PACK, M], F32, name="w_raw", align_bytes=DMA_ALIGN)
         nc.sync.dma_start(
             out=w_raw[:].rearrange("p s j m -> p s (j m)"),
             in_=w.rearrange("(s c) (p j) m -> (c p) s (j m)", s=SETS, j=PACK),
         )
-        x_raw = [load_set(x, s, "x") for s in range(SETS)]
-        res_alone = {}
-        res = []
+        x_raw = [load_x(s) for s in range(SETS)]
+        r_lone = {}
+        r_shared = []
         for s in range(SETS):
             for c in range(SHARED, SIDE):
-                res_alone[s * SIDE + c] = load_r_alone(s * SIDE + c)
-                if s * SIDE + c in (SIDE - 1, G - 1):
-                    res.append(load_r(s))
+                r_lone[s * SIDE + c] = load_r_lone(s * SIDE + c)
+            r_shared.append(load_r_shared(s))
 
         w_bf = []
         for s in range(SETS):
-            t = sb.tile([P, SETS, M // SETS, SETS, PACK], BF16, name="w_bf%d" % s, align_bytes=64)
+            t = sb.tile([P, SETS, M // SETS, SETS, PACK], BF16, name="w_bf%d" % s, align_bytes=MX_ALIGN)
+            nc.vector.memset(t[:SHARED_P], 0.0)
             w_bf.append(t)
-        nc.vector.memset(w_bf[0][: SHARED * ROWS], 0.0)
-        nc.vector.memset(w_bf[1][:], 0.0)
         nc.scalar.copy(
-            out=w_bf[0][SHARED * ROWS :].rearrange("p s q t j -> p s (q t j)").rearrange(
-                "p s (c i j) -> p s c j i", i=4, j=PACK
+            out=w_bf[0][SHARED_P:].rearrange("p s q t j -> p s (q t j)").rearrange(
+                "p s (a b j) -> p s a j b", b=RUN, j=PACK
             ),
-            in_=w_raw[SHARED * ROWS :].rearrange("p s j (c i) -> p s c j i", i=4),
+            in_=w_raw[SHARED_P:].rearrange("p s j (a b) -> p s a j b", b=RUN),
         )
+
+        def round_w_shared(s, copy):
+            copy(
+                out=w_bf[s][:SHARED_P, :, :, s, :],
+                in_=w_raw[:SHARED_P, s].rearrange("p j (q i) -> p i q j", i=SETS),
+            )
 
         def quantize(codes, scales, values):
             nc.vector.quantize_mx(out=codes.bitcast(FP8X4), scales=scales, in_=values)
 
+        def mx_tiles(name, width):
+            codes = sb.tile([P, width], U32, name=name + "_codes", align_bytes=MX_ALIGN)
+            scales = sb.tile([P, width], U8, name=name + "_scales", align_bytes=MX_ALIGN)
+            return codes, scales
+
+        def quantize_w_all_tiles(s):
+            codes, scales = mx_tiles("w%d" % s, SETS * M)
+            quantize(codes[:], scales[:], w_bf[s][:].rearrange("p i q t j -> p (i q t j)"))
+            return codes, scales
+
+        def quantize_w_shared_tiles(s):
+            codes, scales = mx_tiles("w%d" % s, SETS * M)
+            for i in range(SETS):
+                cols = slice(i * M, (i + 1) * M)
+                values = w_bf[s][:SHARED_P, i].rearrange("p q t j -> p (q t j)")
+                quantize(codes[:SHARED_P, cols], scales[:SHARED_P, cols], values)
+            return codes, scales
+
         def round_x(s):
-            lo = sb.tile([P, HALF, PACK], BF16, name="x_lo%d" % s, align_bytes=64)
-            hi = sb.tile([P, HALF, PACK], BF16, name="x_hi%d" % s, align_bytes=64)
+            lo = sb.tile([P, HALF, PACK], BF16, name="x_lo%d" % s, align_bytes=MX_ALIGN)
+            hi = sb.tile([P, HALF, PACK], BF16, name="x_hi%d" % s, align_bytes=MX_ALIGN)
             interleave(nc.vector.tensor_copy, lo[:], x_raw[s][:, :, :HALF])
             interleave(nc.vector.tensor_copy, hi[:, : X_SPLIT - HALF, :], x_raw[s][:, :, HALF:X_SPLIT])
             interleave(nc.scalar.copy, hi[:, X_SPLIT - HALF :, :], x_raw[s][:, :, X_SPLIT:])
             return lo, hi
 
         def quantize_x(s, lo, hi):
-            codes = sb.tile([P, N], U32, name="x_codes%d" % s, align_bytes=64)
-            scales = sb.tile([P, N], U8, name="x_scales%d" % s, align_bytes=64)
+            codes, scales = mx_tiles("x%d" % s, N)
             quantize(codes[:, :HALF], scales[:, :HALF], lo[:].rearrange("p n j -> p (n j)"))
             quantize(codes[:, HALF:], scales[:, HALF:], hi[:].rearrange("p n j -> p (n j)"))
             return codes, scales
 
-        def round_w(s, copy):
-            copy(
-                out=w_bf[s][: SHARED * ROWS, :, :, s, :],
-                in_=w_raw[: SHARED * ROWS, s].rearrange("p j (q i) -> p i q j", i=SETS),
-            )
-
-        def quantize_w(s):
-            codes = sb.tile([P, SETS * M], U32, name="w_codes%d" % s, align_bytes=64)
-            scales = sb.tile([P, SETS * M], U8, name="w_scales%d" % s, align_bytes=64)
-            quantize(codes[:], scales[:], w_bf[s][:].rearrange("p i q t j -> p (i q t j)"))
-            return codes, scales
-
         acc = [[ps.tile([M, N], F32, name="acc%d_%d" % (c, i)) for i in range(SETS)] for c in range(SIDE)]
 
-        def multiply(bank, c, i, wq, xq, start, stop):
+        def multiply(c, i, w_mx, x_mx, start, stop):
             rows = slice(c * ROWS, (c + 1) * ROWS)
             cols = slice(i * M, (i + 1) * M)
             nc.tensor.matmul_mx(
-                out=bank[:],
-                lhsT=wq[0][rows, cols].bitcast(FP8X4),
-                lhsT_scale=wq[1][rows, cols],
-                rhs=xq[0][rows, :].bitcast(FP8X4),
-                rhs_scale=xq[1][rows, :],
+                out=acc[c][i][:],
+                lhsT=w_mx[0][rows, cols].bitcast(FP8X4),
+                lhsT_scale=w_mx[1][rows, cols],
+                rhs=x_mx[0][rows, :].bitcast(FP8X4),
+                rhs_scale=x_mx[1][rows, :],
                 start=start,
                 stop=stop,
             )
 
-        def multiply_set(s, xq):
-            for c in range(SIDE):
-                if c < SHARED:
-                    multiply(acc[c][0], c, 0, wq[s], xq, s == 0, s == SETS - 1)
-                else:
-                    multiply(acc[c][s], c, s, wq[0], xq, True, True)
+        def multiply_set(s, w_sets, x_mx):
             for c in range(SHARED):
-                multiply(acc[c][1], c, 1, wq[s], xq, s == 0, s == SETS - 1)
+                multiply(c, 0, w_sets[s], x_mx, s == 0, s == SETS - 1)
+            for c in range(SHARED, SIDE):
+                multiply(c, s, w_sets[0], x_mx, True, True)
+            for c in range(SHARED):
+                multiply(c, 1, w_sets[s], x_mx, s == 0, s == SETS - 1)
 
-        def relu_add(y, bank, residual):
+        def relu_add_vector(y, sums, residual):
             nc.vector.scalar_tensor_tensor(
-                out=y, in0=bank, scalar=0.0, in1=residual, op0=ALU.max, op1=ALU.add
+                out=y, in0=sums, scalar=0.0, in1=residual, op0=ALU.max, op1=ALU.add
             )
 
-        def finish(c):
-            y = sb.tile([P, SETS * N], F32, name="y%d" % c, align_bytes=256)
-            z = sb.tile([P, HALF], F32, name="z%d" % c, align_bytes=256)
-            last = slice(N + HALF, SETS * N)
-            nc.scalar.activation(out=z[:], in_=acc[c][1][:, HALF:], func=ACT.Relu)
-            nc.gpsimd.tensor_tensor(out=y[:, last], in0=z[:], in1=res[c][:, last], op=ALU.add)
-            relu_add(y[:, :N], acc[c][0][:], res[c][:, :N])
-            relu_add(y[:, N : N + HALF], acc[c][1][:, :HALF], res[c][:, N : N + HALF])
-            nc.sync.dma_start(out=paired(out, c), in_=y[:])
+        def relu_add_scalar_gpsimd(y, sums, residual, name):
+            z = sb.tile([P, HALF], F32, name=name, align_bytes=DMA_ALIGN)
+            nc.scalar.activation(out=z[:], in_=sums, func=ACT.Relu)
+            nc.gpsimd.tensor_tensor(out=y, in0=z[:], in1=residual, op=ALU.add)
 
-        def finish_by_bank(c):
-            for i in range(SETS):
-                cols = slice(i * N, (i + 1) * N)
-                y = sb.tile([P, N], F32, name="y%d_%d" % (c, i), align_bytes=256)
-                relu_add(y[:], acc[c][i][:], res[c][:, cols])
-                nc.sync.dma_start(out=paired(out, c)[:, :, cols], in_=y[:])
-
-        def finish_alone(g):
-            y = sb.tile([P, N], F32, name="y_alone%d" % g, align_bytes=256)
-            relu_add(y[:], acc[g % SIDE][g // SIDE][:], res_alone[g][:])
+        def finish_lone(s, c):
+            g = s * SIDE + c
+            y = sb.tile([P, N], F32, name="y_lone%d" % g, align_bytes=DMA_ALIGN)
+            relu_add_vector(y[:], acc[c][s][:], r_lone[g][:])
             nc.sync.dma_start(out=out[g], in_=y[:])
 
-        def finish_alone_off_vector(g):
-            y = sb.tile([P, N], F32, name="y_alone%d" % g, align_bytes=256)
+        def finish_lone_off_vector(s, c):
+            g = s * SIDE + c
+            y = sb.tile([P, N], F32, name="y_lone%d" % g, align_bytes=DMA_ALIGN)
             for h in range(N // HALF):
                 cols = slice(h * HALF, (h + 1) * HALF)
-                z = sb.tile([P, HALF], F32, name="z_alone%d_%d" % (g, h), align_bytes=256)
-                nc.scalar.activation(out=z[:], in_=acc[g % SIDE][g // SIDE][:, cols], func=ACT.Relu)
-                nc.gpsimd.tensor_tensor(out=y[:, cols], in0=z[:], in1=res_alone[g][:, cols], op=ALU.add)
+                relu_add_scalar_gpsimd(y[:, cols], acc[c][s][:, cols], r_lone[g][:, cols], "z%d_%d" % (g, h))
             nc.sync.dma_start(out=out[g], in_=y[:])
 
-        round_w(0, nc.scalar.copy)
-        round_w(1, nc.vector.tensor_copy)
-        wq = {1: quantize_w(1)}
+        def finish_shared_by_bank(c):
+            for i in range(SETS):
+                cols = slice(i * N, (i + 1) * N)
+                y = sb.tile([P, N], F32, name="y_shared%d_%d" % (c, i), align_bytes=DMA_ALIGN)
+                relu_add_vector(y[:], acc[c][i][:], r_shared[c][:, cols])
+                nc.sync.dma_start(out=paired(out, c)[:, :, cols], in_=y[:])
+
+        def finish_shared(c):
+            y = sb.tile([P, SETS * N], F32, name="y_shared%d" % c, align_bytes=DMA_ALIGN)
+            lower = slice(N, N + HALF)
+            upper = slice(N + HALF, SETS * N)
+            relu_add_scalar_gpsimd(y[:, upper], acc[c][1][:, HALF:], r_shared[c][:, upper], "z_shared%d" % c)
+            relu_add_vector(y[:, :N], acc[c][0][:], r_shared[c][:, :N])
+            relu_add_vector(y[:, lower], acc[c][1][:, :HALF], r_shared[c][:, lower])
+            nc.sync.dma_start(out=paired(out, c), in_=y[:])
+
+        round_w_shared(0, nc.scalar.copy)
+        round_w_shared(1, nc.vector.tensor_copy)
+        w_set1 = quantize_w_shared_tiles(1)
         x_bf = round_x(0)
-        wq[0] = quantize_w(0)
-        multiply_set(0, quantize_x(0, *x_bf))
-        multiply_set(1, quantize_x(1, *round_x(1)))
-        finish_alone(2)
-        finish_alone(3)
-        finish_by_bank(0)
-        finish_alone_off_vector(6)
-        finish_alone(7)
-        finish(1)
+        w_sets = [quantize_w_all_tiles(0), w_set1]
+        multiply_set(0, w_sets, quantize_x(0, *x_bf))
+        multiply_set(1, w_sets, quantize_x(1, *round_x(1)))
+
+        for c in range(SHARED, SIDE):
+            finish_lone(0, c)
+        finish_shared_by_bank(0)
+        finish_lone_off_vector(1, SHARED)
+        finish_lone(1, SHARED + 1)
+        finish_shared(1)

@@ -63,12 +63,13 @@ def tile_rows_glin_relu_res_kernel(tc, x, w, r, out):
             nc.sync.dma_start(out=t[:], in_=r[g])
             return t
 
+        x_raw = [load_x(0)]
         w_raw = sb.tile([P, SETS, PACK, M], F32, name="w_raw", align_bytes=DMA_ALIGN)
         nc.sync.dma_start(
             out=w_raw[:].rearrange("p s j m -> p s (j m)"),
             in_=w.rearrange("(s c) (p j) m -> (c p) s (j m)", s=SETS, j=PACK),
         )
-        x_raw = [load_x(s) for s in range(SETS)]
+        x_raw.append(load_x(1))
         r_lone = {}
         r_shared = []
         for s in range(SETS):
@@ -81,12 +82,14 @@ def tile_rows_glin_relu_res_kernel(tc, x, w, r, out):
             t = sb.tile([P, SETS, M // SETS, SETS, PACK], BF16, name="w_bf%d" % s, align_bytes=MX_ALIGN)
             nc.vector.memset(t[:SHARED_P], 0.0)
             w_bf.append(t)
-        nc.scalar.copy(
-            out=w_bf[0][SHARED_P:].rearrange("p s q t j -> p s (q t j)").rearrange(
-                "p s (a b j) -> p s a j b", b=RUN, j=PACK
-            ),
-            in_=w_raw[SHARED_P:].rearrange("p s j (a b) -> p s a j b", b=RUN),
-        )
+
+        def round_w_lone():
+            nc.scalar.copy(
+                out=w_bf[0][SHARED_P:].rearrange("p s q t j -> p s (q t j)").rearrange(
+                    "p s (a b j) -> p s a j b", b=RUN, j=PACK
+                ),
+                in_=w_raw[SHARED_P:].rearrange("p s j (a b) -> p s a j b", b=RUN),
+            )
 
         def round_w_shared(s, copy):
             copy(
@@ -192,12 +195,13 @@ def tile_rows_glin_relu_res_kernel(tc, x, w, r, out):
             relu_add_vector(y[:, lower], acc[c][1][:, :HALF], r_shared[c][:, lower])
             nc.sync.dma_start(out=paired(out, c), in_=y[:])
 
-        round_w_shared(0, nc.scalar.copy)
+        x_set0 = quantize_x(0, *round_x(0))
+        round_w_lone()
         round_w_shared(1, nc.vector.tensor_copy)
+        round_w_shared(0, nc.vector.tensor_copy)
         w_set1 = quantize_w_shared_tiles(1)
-        x_bf = round_x(0)
         w_sets = [quantize_w_all_tiles(0), w_set1]
-        multiply_set(0, w_sets, quantize_x(0, *x_bf))
+        multiply_set(0, w_sets, x_set0)
         multiply_set(1, w_sets, quantize_x(1, *round_x(1)))
 
         for c in range(SHARED, SIDE):

@@ -18,13 +18,13 @@ PACK = 4
 ROWS = D // PACK
 SIDE = P // ROWS
 SETS = G // SIDE
-SHARED = SIDE // 2
-SHARED_P = SHARED * ROWS
 HALF = N // 2
 RUN = 4
 X_SPLIT = 304
 MX_ALIGN = 64
 DMA_ALIGN = 256
+STORES = (1, 1, 2, 2, 2)
+GPSIMD_FROM = {3: 0, 5: 0, 7: 352}
 
 
 def interleave(copy, dst, src):
@@ -34,8 +34,13 @@ def interleave(copy, dst, src):
     )
 
 
-def paired(t, c):
-    return t.rearrange("(s c) (q i) n -> c q s (i n)", s=SETS, i=SETS)[c]
+def batches(sizes):
+    first = 0
+    result = []
+    for size in sizes:
+        result.append(range(first, first + size))
+        first = first + size
+    return result
 
 
 def tile_rows_glin_relu_res_kernel(tc, x, w, r, out):
@@ -53,15 +58,13 @@ def tile_rows_glin_relu_res_kernel(tc, x, w, r, out):
             )
             return t
 
-        def load_r_shared(c):
-            t = sb.tile([P, SETS * N], F32, name="r_shared%d" % c, align_bytes=DMA_ALIGN)
-            nc.sync.dma_start(out=t[:], in_=paired(r, c))
-            return t
+        residual = {}
 
-        def load_r_lone(g):
-            t = sb.tile([P, N], F32, name="r_lone%d" % g, align_bytes=DMA_ALIGN)
-            nc.sync.dma_start(out=t[:], in_=r[g])
-            return t
+        def load_r(queue, groups):
+            for g in groups:
+                t = sb.tile([P, N], F32, name="r%d" % g, align_bytes=DMA_ALIGN)
+                queue.dma_start(out=t[:], in_=r[g])
+                residual[g] = t
 
         x_raw = [load_x(0)]
         w_raw = sb.tile([P, SETS, PACK, M], F32, name="w_raw", align_bytes=DMA_ALIGN)
@@ -70,32 +73,7 @@ def tile_rows_glin_relu_res_kernel(tc, x, w, r, out):
             in_=w.rearrange("(s c) (p j) m -> (c p) s (j m)", s=SETS, j=PACK),
         )
         x_raw.append(load_x(1))
-        r_lone = {}
-        r_shared = []
-        for s in range(SETS):
-            for c in range(SHARED, SIDE):
-                r_lone[s * SIDE + c] = load_r_lone(s * SIDE + c)
-            r_shared.append(load_r_shared(s))
-
-        w_bf = []
-        for s in range(SETS):
-            t = sb.tile([P, SETS, M // SETS, SETS, PACK], BF16, name="w_bf%d" % s, align_bytes=MX_ALIGN)
-            nc.vector.memset(t[:SHARED_P], 0.0)
-            w_bf.append(t)
-
-        def round_w_lone():
-            nc.scalar.copy(
-                out=w_bf[0][SHARED_P:].rearrange("p s q t j -> p s (q t j)").rearrange(
-                    "p s (a b j) -> p s a j b", b=RUN, j=PACK
-                ),
-                in_=w_raw[SHARED_P:].rearrange("p s j (a b) -> p s a j b", b=RUN),
-            )
-
-        def round_w_shared(s, copy):
-            copy(
-                out=w_bf[s][:SHARED_P, :, :, s, :],
-                in_=w_raw[:SHARED_P, s].rearrange("p j (q i) -> p i q j", i=SETS),
-            )
+        load_r(nc.sync, range(0, G, 2))
 
         def quantize(codes, scales, values):
             nc.vector.quantize_mx(out=codes.bitcast(FP8X4), scales=scales, in_=values)
@@ -103,19 +81,6 @@ def tile_rows_glin_relu_res_kernel(tc, x, w, r, out):
         def mx_tiles(name, width):
             codes = sb.tile([P, width], U32, name=name + "_codes", align_bytes=MX_ALIGN)
             scales = sb.tile([P, width], U8, name=name + "_scales", align_bytes=MX_ALIGN)
-            return codes, scales
-
-        def quantize_w_all_tiles(s):
-            codes, scales = mx_tiles("w%d" % s, SETS * M)
-            quantize(codes[:], scales[:], w_bf[s][:].rearrange("p i q t j -> p (i q t j)"))
-            return codes, scales
-
-        def quantize_w_shared_tiles(s):
-            codes, scales = mx_tiles("w%d" % s, SETS * M)
-            for i in range(SETS):
-                cols = slice(i * M, (i + 1) * M)
-                values = w_bf[s][:SHARED_P, i].rearrange("p q t j -> p (q t j)")
-                quantize(codes[:SHARED_P, cols], scales[:SHARED_P, cols], values)
             return codes, scales
 
         def round_x(s):
@@ -132,81 +97,65 @@ def tile_rows_glin_relu_res_kernel(tc, x, w, r, out):
             quantize(codes[:, HALF:], scales[:, HALF:], hi[:].rearrange("p n j -> p (n j)"))
             return codes, scales
 
-        acc = [[ps.tile([M, N], F32, name="acc%d_%d" % (c, i)) for i in range(SETS)] for c in range(SIDE)]
+        def prepare_w():
+            w_bf = sb.tile([P, SETS, M, PACK], BF16, name="w_bf", align_bytes=MX_ALIGN)
+            interleave(nc.vector.tensor_copy, w_bf[:, 0], w_raw[:, 0])
+            interleave(nc.scalar.copy, w_bf[:, 1], w_raw[:, 1])
+            codes, scales = mx_tiles("w", SETS * M)
+            quantize(codes[:], scales[:], w_bf[:].rearrange("p s m j -> p (s m j)"))
+            return codes, scales
 
-        def multiply(c, i, w_mx, x_mx, start, stop):
-            rows = slice(c * ROWS, (c + 1) * ROWS)
-            cols = slice(i * M, (i + 1) * M)
-            nc.tensor.matmul_mx(
-                out=acc[c][i][:],
-                lhsT=w_mx[0][rows, cols].bitcast(FP8X4),
-                lhsT_scale=w_mx[1][rows, cols],
-                rhs=x_mx[0][rows, :].bitcast(FP8X4),
-                rhs_scale=x_mx[1][rows, :],
-                start=start,
-                stop=stop,
-            )
+        acc = [ps.tile([M, N], F32, name="acc%d" % g) for g in range(G)]
 
-        def multiply_set(s, w_sets, x_mx):
-            for c in range(SHARED):
-                multiply(c, 0, w_sets[s], x_mx, s == 0, s == SETS - 1)
-            for c in range(SHARED, SIDE):
-                multiply(c, s, w_sets[0], x_mx, True, True)
-            for c in range(SHARED):
-                multiply(c, 1, w_sets[s], x_mx, s == 0, s == SETS - 1)
+        def multiply_set(s, w_mx, x_mx):
+            cols = slice(s * M, (s + 1) * M)
+            for c in range(SIDE):
+                rows = slice(c * ROWS, (c + 1) * ROWS)
+                nc.tensor.matmul_mx(
+                    out=acc[s * SIDE + c][:],
+                    lhsT=w_mx[0][rows, cols].bitcast(FP8X4),
+                    lhsT_scale=w_mx[1][rows, cols],
+                    rhs=x_mx[0][rows, :].bitcast(FP8X4),
+                    rhs_scale=x_mx[1][rows, :],
+                    start=True,
+                    stop=True,
+                )
 
-        def relu_add_vector(y, sums, residual):
-            nc.vector.scalar_tensor_tensor(
-                out=y, in0=sums, scalar=0.0, in1=residual, op0=ALU.max, op1=ALU.add
-            )
-
-        def relu_add_scalar_gpsimd(y, sums, residual, name):
-            z = sb.tile([P, HALF], F32, name=name, align_bytes=DMA_ALIGN)
-            nc.scalar.activation(out=z[:], in_=sums, func=ACT.Relu)
-            nc.gpsimd.tensor_tensor(out=y, in0=z[:], in1=residual, op=ALU.add)
-
-        def finish_lone(s, c):
-            g = s * SIDE + c
-            y = sb.tile([P, N], F32, name="y_lone%d" % g, align_bytes=DMA_ALIGN)
-            relu_add_vector(y[:], acc[c][s][:], r_lone[g][:])
-            nc.sync.dma_start(out=out[g], in_=y[:])
-
-        def finish_lone_off_vector(s, c):
-            g = s * SIDE + c
-            y = sb.tile([P, N], F32, name="y_lone%d" % g, align_bytes=DMA_ALIGN)
-            for h in range(N // HALF):
-                cols = slice(h * HALF, (h + 1) * HALF)
-                relu_add_scalar_gpsimd(y[:, cols], acc[c][s][:, cols], r_lone[g][:, cols], "z%d_%d" % (g, h))
-            nc.sync.dma_start(out=out[g], in_=y[:])
-
-        def finish_shared_by_bank(c):
-            for i in range(SETS):
-                cols = slice(i * N, (i + 1) * N)
-                y = sb.tile([P, N], F32, name="y_shared%d_%d" % (c, i), align_bytes=DMA_ALIGN)
-                relu_add_vector(y[:], acc[c][i][:], r_shared[c][:, cols])
-                nc.sync.dma_start(out=paired(out, c)[:, :, cols], in_=y[:])
-
-        def finish_shared(c):
-            y = sb.tile([P, SETS * N], F32, name="y_shared%d" % c, align_bytes=DMA_ALIGN)
-            lower = slice(N, N + HALF)
-            upper = slice(N + HALF, SETS * N)
-            relu_add_scalar_gpsimd(y[:, upper], acc[c][1][:, HALF:], r_shared[c][:, upper], "z_shared%d" % c)
-            relu_add_vector(y[:, :N], acc[c][0][:], r_shared[c][:, :N])
-            relu_add_vector(y[:, lower], acc[c][1][:, :HALF], r_shared[c][:, lower])
-            nc.sync.dma_start(out=paired(out, c), in_=y[:])
+        def relu_on_scalar(g):
+            first = GPSIMD_FROM[g]
+            z = sb.tile([P, N - first], F32, name="z%d" % g, align_bytes=DMA_ALIGN)
+            nc.scalar.activation(out=z[:], in_=acc[g][:, first:], func=ACT.Relu)
+            return z
 
         x_set0 = quantize_x(0, *round_x(0))
-        round_w_lone()
-        round_w_shared(1, nc.vector.tensor_copy)
-        round_w_shared(0, nc.vector.tensor_copy)
-        w_set1 = quantize_w_shared_tiles(1)
-        w_sets = [quantize_w_all_tiles(0), w_set1]
-        multiply_set(0, w_sets, x_set0)
-        multiply_set(1, w_sets, quantize_x(1, *round_x(1)))
+        w_mx = prepare_w()
+        load_r(nc.scalar, range(1, G - 1, 2))
+        multiply_set(0, w_mx, x_set0)
+        x_set1 = round_x(1)
+        load_r(nc.scalar, [G - 1])
+        multiply_set(1, w_mx, quantize_x(1, *x_set1))
 
-        for c in range(SHARED, SIDE):
-            finish_lone(0, c)
-        finish_shared_by_bank(0)
-        finish_lone_off_vector(1, SHARED)
-        finish_lone(1, SHARED + 1)
-        finish_shared(1)
+        relu = {3: relu_on_scalar(3)}
+        for k, groups in enumerate(batches(STORES)):
+            y = sb.tile([P, len(groups), N], F32, name="y%d" % groups.start, align_bytes=DMA_ALIGN)
+            for g in groups:
+                row = y[:, g - groups.start, :]
+                first = GPSIMD_FROM.get(g, N)
+                if first < N:
+                    nc.gpsimd.tensor_tensor(
+                        out=row[:, first:], in0=relu[g][:], in1=residual[g][:, first:], op=ALU.add
+                    )
+                if first > 0:
+                    nc.vector.scalar_tensor_tensor(
+                        out=row[:, :first],
+                        in0=acc[g][:, :first],
+                        scalar=0.0,
+                        in1=residual[g][:, :first],
+                        op0=ALU.max,
+                        op1=ALU.add,
+                    )
+            queue = nc.scalar if k % 2 else nc.sync
+            queue.dma_start(out=out[groups.start : groups.stop].rearrange("g m n -> m g n"), in_=y[:])
+            if k == 1:
+                relu[5] = relu_on_scalar(5)
+                relu[7] = relu_on_scalar(7)

@@ -24,7 +24,7 @@ X_SPLIT = 304
 MX_ALIGN = 64
 DMA_ALIGN = 256
 STORES = (1, 1, 2, 2, 2)
-GPSIMD_FROM = {3: 0, 5: 0, 7: 352}
+GPSIMD_FROM = {2: 0}
 
 
 def interleave(copy, dst, src):
@@ -73,7 +73,7 @@ def tile_rows_glin_relu_res_kernel(tc, x, w, r, out):
             in_=w.rearrange("(s c) (p j) m -> (c p) s (j m)", s=SETS, j=PACK),
         )
         x_raw.append(load_x(1))
-        load_r(nc.sync, range(0, G, 2))
+        load_r(nc.sync, range(G))
 
         def quantize(codes, scales, values):
             nc.vector.quantize_mx(out=codes.bitcast(FP8X4), scales=scales, in_=values)
@@ -129,13 +129,11 @@ def tile_rows_glin_relu_res_kernel(tc, x, w, r, out):
 
         x_set0 = quantize_x(0, *round_x(0))
         w_mx = prepare_w()
-        load_r(nc.scalar, range(1, G - 1, 2))
         multiply_set(0, w_mx, x_set0)
         x_set1 = round_x(1)
-        load_r(nc.scalar, [G - 1])
         multiply_set(1, w_mx, quantize_x(1, *x_set1))
 
-        relu = {3: relu_on_scalar(3)}
+        relu = {g: relu_on_scalar(g) for g in GPSIMD_FROM}
         for k, groups in enumerate(batches(STORES)):
             y = sb.tile([P, len(groups), N], F32, name="y%d" % groups.start, align_bytes=DMA_ALIGN)
             for g in groups:
@@ -156,6 +154,3 @@ def tile_rows_glin_relu_res_kernel(tc, x, w, r, out):
                     )
             queue = nc.scalar if k % 2 else nc.sync
             queue.dma_start(out=out[groups.start : groups.stop].rearrange("g m n -> m g n"), in_=y[:])
-            if k == 1:
-                relu[5] = relu_on_scalar(5)
-                relu[7] = relu_on_scalar(7)

@@ -11,7 +11,6 @@ U32 = mybir.dt.uint32
 U8 = mybir.dt.uint8
 FP8X4 = mybir.dt.float8_e4m3fn_x4
 ALU = mybir.AluOpType
-ACT = mybir.ActivationFunctionType
 
 P = 128
 PACK = 4
@@ -20,18 +19,10 @@ SIDE = P // ROWS
 SETS = G // SIDE
 HALF = N // 2
 RUN = 4
-X_SPLIT = 304
 MX_ALIGN = 64
 DMA_ALIGN = 256
-STORES = (1, 1, 2, 2, 2)
-GPSIMD_FROM = {2: 0}
-
-
-def interleave(copy, dst, src):
-    copy(
-        out=dst.rearrange("p (a b) j -> p a j b", b=RUN),
-        in_=src.rearrange("p j (a b) -> p a j b", b=RUN),
-    )
+R_LOADS = (2, 2, 2, 1, 1)
+STORES = (1,) * G
 
 
 def batches(sizes):
@@ -50,64 +41,56 @@ def tile_rows_glin_relu_res_kernel(tc, x, w, r, out):
         ps = ctx.enter_context(tc.psum_pool(name="ps", bufs=1))
         ctx.enter_context(tc.manual_schedule())
 
-        def load_x(s):
-            t = sb.tile([P, PACK, N], F32, name="x_raw%d" % s, align_bytes=DMA_ALIGN)
-            nc.sync.dma_start(
-                out=t[:].rearrange("p j n -> p (j n)"),
-                in_=x[s * SIDE : (s + 1) * SIDE].rearrange("c (p j) n -> (c p) (j n)", j=PACK),
-            )
-            return t
-
-        residual = {}
-
-        def load_r(queue, groups):
-            for g in groups:
-                t = sb.tile([P, N], F32, name="r%d" % g, align_bytes=DMA_ALIGN)
-                queue.dma_start(out=t[:], in_=r[g])
-                residual[g] = t
-
-        x_raw = [load_x(0)]
         w_raw = sb.tile([P, SETS, PACK, M], F32, name="w_raw", align_bytes=DMA_ALIGN)
         nc.sync.dma_start(
             out=w_raw[:].rearrange("p s j m -> p s (j m)"),
             in_=w.rearrange("(s c) (p j) m -> (c p) s (j m)", s=SETS, j=PACK),
         )
-        x_raw.append(load_x(1))
-        load_r(nc.sync, range(G))
+        x_raw = []
+        for s in range(SETS):
+            t = sb.tile([P, PACK, N], F32, name="x_raw%d" % s, align_bytes=DMA_ALIGN)
+            nc.sync.dma_start(
+                out=t[:].rearrange("p j n -> p (j n)"),
+                in_=x[s * SIDE : (s + 1) * SIDE].rearrange("c (p j) n -> (c p) (j n)", j=PACK),
+            )
+            x_raw.append(t)
+        residual = {}
+        for groups in batches(R_LOADS):
+            t = sb.tile([P, len(groups), N], F32, name="r%d" % groups.start, align_bytes=DMA_ALIGN)
+            nc.sync.dma_start(out=t[:], in_=r[groups.start : groups.stop].rearrange("g m n -> m g n"))
+            for g in groups:
+                residual[g] = t[:, g - groups.start, :]
 
-        def quantize(codes, scales, values):
-            nc.vector.quantize_mx(out=codes.bitcast(FP8X4), scales=scales, in_=values)
+        def round_halves(name, halves):
+            rounded = []
+            for h, src in enumerate(halves):
+                dst = sb.tile([P, src.shape[2], PACK], BF16, name="%s_bf%d" % (name, h), align_bytes=MX_ALIGN)
+                nc.vector.tensor_copy(
+                    out=dst[:].rearrange("p (a b) j -> p a j b", b=RUN),
+                    in_=src.rearrange("p j (a b) -> p a j b", b=RUN),
+                )
+                rounded.append(dst)
+            return rounded
 
-        def mx_tiles(name, width):
-            codes = sb.tile([P, width], U32, name=name + "_codes", align_bytes=MX_ALIGN)
-            scales = sb.tile([P, width], U8, name=name + "_scales", align_bytes=MX_ALIGN)
+        def quantize_halves(name, rounded):
+            width = rounded[0].shape[1]
+            codes = sb.tile([P, 2 * width], U32, name=name + "_codes", align_bytes=MX_ALIGN)
+            scales = sb.tile([P, 2 * width], U8, name=name + "_scales", align_bytes=MX_ALIGN)
+            for h, values in enumerate(rounded):
+                cols = slice(h * width, (h + 1) * width)
+                nc.vector.quantize_mx(
+                    out=codes[:, cols].bitcast(FP8X4),
+                    scales=scales[:, cols],
+                    in_=values[:].rearrange("p n j -> p (n j)"),
+                )
             return codes, scales
 
-        def round_x(s):
-            lo = sb.tile([P, HALF, PACK], BF16, name="x_lo%d" % s, align_bytes=MX_ALIGN)
-            hi = sb.tile([P, HALF, PACK], BF16, name="x_hi%d" % s, align_bytes=MX_ALIGN)
-            interleave(nc.vector.tensor_copy, lo[:], x_raw[s][:, :, :HALF])
-            interleave(nc.vector.tensor_copy, hi[:, : X_SPLIT - HALF, :], x_raw[s][:, :, HALF:X_SPLIT])
-            interleave(nc.scalar.copy, hi[:, X_SPLIT - HALF :, :], x_raw[s][:, :, X_SPLIT:])
-            return lo, hi
-
-        def quantize_x(s, lo, hi):
-            codes, scales = mx_tiles("x%d" % s, N)
-            quantize(codes[:, :HALF], scales[:, :HALF], lo[:].rearrange("p n j -> p (n j)"))
-            quantize(codes[:, HALF:], scales[:, HALF:], hi[:].rearrange("p n j -> p (n j)"))
-            return codes, scales
-
-        def prepare_w():
-            w_bf = sb.tile([P, SETS, M, PACK], BF16, name="w_bf", align_bytes=MX_ALIGN)
-            interleave(nc.vector.tensor_copy, w_bf[:, 0], w_raw[:, 0])
-            interleave(nc.scalar.copy, w_bf[:, 1], w_raw[:, 1])
-            codes, scales = mx_tiles("w", SETS * M)
-            quantize(codes[:], scales[:], w_bf[:].rearrange("p s m j -> p (s m j)"))
-            return codes, scales
+        w_mx = quantize_halves("w", round_halves("w", [w_raw[:, s] for s in range(SETS)]))
 
         acc = [ps.tile([M, N], F32, name="acc%d" % g) for g in range(G)]
-
-        def multiply_set(s, w_mx, x_mx):
+        for s in range(SETS):
+            name = "x%d" % s
+            x_mx = quantize_halves(name, round_halves(name, [x_raw[s][:, :, :HALF], x_raw[s][:, :, HALF:]]))
             cols = slice(s * M, (s + 1) * M)
             for c in range(SIDE):
                 rows = slice(c * ROWS, (c + 1) * ROWS)
@@ -121,36 +104,15 @@ def tile_rows_glin_relu_res_kernel(tc, x, w, r, out):
                     stop=True,
                 )
 
-        def relu_on_scalar(g):
-            first = GPSIMD_FROM[g]
-            z = sb.tile([P, N - first], F32, name="z%d" % g, align_bytes=DMA_ALIGN)
-            nc.scalar.activation(out=z[:], in_=acc[g][:, first:], func=ACT.Relu)
-            return z
-
-        x_set0 = quantize_x(0, *round_x(0))
-        w_mx = prepare_w()
-        multiply_set(0, w_mx, x_set0)
-        x_set1 = round_x(1)
-        multiply_set(1, w_mx, quantize_x(1, *x_set1))
-
-        relu = {g: relu_on_scalar(g) for g in GPSIMD_FROM}
-        for k, groups in enumerate(batches(STORES)):
+        for groups in batches(STORES):
             y = sb.tile([P, len(groups), N], F32, name="y%d" % groups.start, align_bytes=DMA_ALIGN)
             for g in groups:
-                row = y[:, g - groups.start, :]
-                first = GPSIMD_FROM.get(g, N)
-                if first < N:
-                    nc.gpsimd.tensor_tensor(
-                        out=row[:, first:], in0=relu[g][:], in1=residual[g][:, first:], op=ALU.add
-                    )
-                if first > 0:
-                    nc.vector.scalar_tensor_tensor(
-                        out=row[:, :first],
-                        in0=acc[g][:, :first],
-                        scalar=0.0,
-                        in1=residual[g][:, :first],
-                        op0=ALU.max,
-                        op1=ALU.add,
-                    )
-            queue = nc.scalar if k % 2 else nc.sync
-            queue.dma_start(out=out[groups.start : groups.stop].rearrange("g m n -> m g n"), in_=y[:])
+                nc.vector.scalar_tensor_tensor(
+                    out=y[:, g - groups.start, :],
+                    in0=acc[g][:],
+                    scalar=0.0,
+                    in1=residual[g],
+                    op0=ALU.max,
+                    op1=ALU.add,
+                )
+            nc.sync.dma_start(out=out[groups.start : groups.stop].rearrange("g m n -> m g n"), in_=y[:])

@@ -21,7 +21,7 @@ HALF = N // 2
 RUN = 4
 MX_ALIGN = 64
 DMA_ALIGN = 256
-R_LOADS = (2, 2, 2, 1, 1)
+R_LOADS = (2, 2, 2, 2)
 STORES = (1,) * G
 
 
@@ -41,11 +41,14 @@ def tile_rows_glin_relu_res_kernel(tc, x, w, r, out):
         ps = ctx.enter_context(tc.psum_pool(name="ps", bufs=1))
         ctx.enter_context(tc.manual_schedule())
 
-        w_raw = sb.tile([P, SETS, PACK, M], F32, name="w_raw", align_bytes=DMA_ALIGN)
-        nc.sync.dma_start(
-            out=w_raw[:].rearrange("p s j m -> p s (j m)"),
-            in_=w.rearrange("(s c) (p j) m -> (c p) s (j m)", s=SETS, j=PACK),
-        )
+        w_raw = []
+        for s, queue in enumerate((nc.sync, nc.scalar)):
+            t = sb.tile([P, PACK, M], F32, name="w_raw%d" % s, align_bytes=DMA_ALIGN)
+            queue.dma_start(
+                out=t[:].rearrange("p j m -> p (j m)"),
+                in_=w[s * SIDE : (s + 1) * SIDE].rearrange("c (p j) m -> (c p) (j m)", j=PACK),
+            )
+            w_raw.append(t)
         x_raw = []
         for s in range(SETS):
             t = sb.tile([P, PACK, N], F32, name="x_raw%d" % s, align_bytes=DMA_ALIGN)
@@ -85,7 +88,7 @@ def tile_rows_glin_relu_res_kernel(tc, x, w, r, out):
                 )
             return codes, scales
 
-        w_mx = quantize_halves("w", round_halves("w", [w_raw[:, s] for s in range(SETS)]))
+        w_mx = quantize_halves("w", round_halves("w", [t[:] for t in w_raw]))
 
         acc = [ps.tile([M, N], F32, name="acc%d" % g) for g in range(G)]
         for s in range(SETS):

@@ -21,8 +21,17 @@ HALF = N // 2
 RUN = 4
 MX_ALIGN = 64
 DMA_ALIGN = 256
-R_LOADS = (2, 2, 2, 2)
+X_SPLIT = 304
+EARLY = 2
+R_LOADS = (EARLY, 2, 2, 1, 1)
 STORES = (1,) * G
+
+
+def interleave(copy, dst, src):
+    copy(
+        out=dst.rearrange("p (a b) j -> p a j b", b=RUN),
+        in_=src.rearrange("p j (a b) -> p a j b", b=RUN),
+    )
 
 
 def batches(sizes):
@@ -41,39 +50,34 @@ def tile_rows_glin_relu_res_kernel(tc, x, w, r, out):
         ps = ctx.enter_context(tc.psum_pool(name="ps", bufs=1))
         ctx.enter_context(tc.manual_schedule())
 
-        w_raw = []
-        for s, queue in enumerate((nc.sync, nc.scalar)):
-            t = sb.tile([P, PACK, M], F32, name="w_raw%d" % s, align_bytes=DMA_ALIGN)
-            queue.dma_start(
-                out=t[:].rearrange("p j m -> p (j m)"),
-                in_=w[s * SIDE : (s + 1) * SIDE].rearrange("c (p j) m -> (c p) (j m)", j=PACK),
-            )
-            w_raw.append(t)
-        x_raw = []
-        for s in range(SETS):
+        w_raw = sb.tile([P, SETS, PACK, M], F32, name="w_raw", align_bytes=DMA_ALIGN)
+        nc.sync.dma_start(
+            out=w_raw[:].rearrange("p s j m -> p s (j m)"),
+            in_=w.rearrange("(s c) (p j) m -> (c p) s (j m)", s=SETS, j=PACK),
+        )
+
+        def load_x(s):
             t = sb.tile([P, PACK, N], F32, name="x_raw%d" % s, align_bytes=DMA_ALIGN)
             nc.sync.dma_start(
                 out=t[:].rearrange("p j n -> p (j n)"),
                 in_=x[s * SIDE : (s + 1) * SIDE].rearrange("c (p j) n -> (c p) (j n)", j=PACK),
             )
-            x_raw.append(t)
+            return t
+
         residual = {}
-        for groups in batches(R_LOADS):
+
+        def load_r(groups):
             t = sb.tile([P, len(groups), N], F32, name="r%d" % groups.start, align_bytes=DMA_ALIGN)
             nc.sync.dma_start(out=t[:], in_=r[groups.start : groups.stop].rearrange("g m n -> m g n"))
             for g in groups:
                 residual[g] = t[:, g - groups.start, :]
 
-        def round_halves(name, halves):
-            rounded = []
-            for h, src in enumerate(halves):
-                dst = sb.tile([P, src.shape[2], PACK], BF16, name="%s_bf%d" % (name, h), align_bytes=MX_ALIGN)
-                nc.vector.tensor_copy(
-                    out=dst[:].rearrange("p (a b) j -> p a j b", b=RUN),
-                    in_=src.rearrange("p j (a b) -> p a j b", b=RUN),
-                )
-                rounded.append(dst)
-            return rounded
+        r_batches = batches(R_LOADS)
+        x_raw = [load_x(0)]
+        load_r(r_batches[0])
+        x_raw.append(load_x(1))
+        for groups in r_batches[1:]:
+            load_r(groups)
 
         def quantize_halves(name, rounded):
             width = rounded[0].shape[1]
@@ -88,12 +92,23 @@ def tile_rows_glin_relu_res_kernel(tc, x, w, r, out):
                 )
             return codes, scales
 
-        w_mx = quantize_halves("w", round_halves("w", [t[:] for t in w_raw]))
+        w_bf = [sb.tile([P, M, PACK], BF16, name="w_bf%d" % s, align_bytes=MX_ALIGN) for s in range(SETS)]
+        for s in range(SETS):
+            interleave(nc.vector.tensor_copy, w_bf[s][:], w_raw[:, s])
+        w_mx = quantize_halves("w", w_bf)
 
         acc = [ps.tile([M, N], F32, name="acc%d" % g) for g in range(G)]
-        for s in range(SETS):
-            name = "x%d" % s
-            x_mx = quantize_halves(name, round_halves(name, [x_raw[s][:, :, :HALF], x_raw[s][:, :, HALF:]]))
+
+        def round_x(s):
+            lo = sb.tile([P, HALF, PACK], BF16, name="x_lo%d" % s, align_bytes=MX_ALIGN)
+            hi = sb.tile([P, HALF, PACK], BF16, name="x_hi%d" % s, align_bytes=MX_ALIGN)
+            interleave(nc.vector.tensor_copy, lo[:], x_raw[s][:, :, :HALF])
+            interleave(nc.vector.tensor_copy, hi[:, : X_SPLIT - HALF, :], x_raw[s][:, :, HALF:X_SPLIT])
+            interleave(nc.scalar.copy, hi[:, X_SPLIT - HALF :, :], x_raw[s][:, :, X_SPLIT:])
+            return [lo, hi]
+
+        def multiply_set(s, rounded):
+            x_mx = quantize_halves("x%d" % s, rounded)
             cols = slice(s * M, (s + 1) * M)
             for c in range(SIDE):
                 rows = slice(c * ROWS, (c + 1) * ROWS)
@@ -107,7 +122,7 @@ def tile_rows_glin_relu_res_kernel(tc, x, w, r, out):
                     stop=True,
                 )
 
-        for groups in batches(STORES):
+        def finish(groups):
             y = sb.tile([P, len(groups), N], F32, name="y%d" % groups.start, align_bytes=DMA_ALIGN)
             for g in groups:
                 nc.vector.scalar_tensor_tensor(
@@ -118,4 +133,17 @@ def tile_rows_glin_relu_res_kernel(tc, x, w, r, out):
                     op0=ALU.max,
                     op1=ALU.add,
                 )
-            nc.sync.dma_start(out=out[groups.start : groups.stop].rearrange("g m n -> m g n"), in_=y[:])
+            return y
+
+        def store(queue, groups, y):
+            queue.dma_start(out=out[groups.start : groups.stop].rearrange("g m n -> m g n"), in_=y[:])
+
+        stores = batches(STORES)
+        multiply_set(0, round_x(0))
+        store(nc.scalar, stores[0], finish(stores[0]))
+        second = finish(stores[1])
+        rounded = round_x(1)
+        store(nc.scalar, stores[1], second)
+        multiply_set(1, rounded)
+        for groups in stores[EARLY:]:
+            store(nc.sync, groups, finish(groups))

from contextlib import ExitStack

import concourse.mybir as mybir

G, D, M, N = 8, 128, 128, 512
FLOPS = 2 * G * D * M * N

F32 = mybir.dt.float32
BF16 = mybir.dt.bfloat16
U32 = mybir.dt.uint32
U8 = mybir.dt.uint8
FP8X4 = mybir.dt.float8_e4m3fn_x4
ALU = mybir.AluOpType

P = 128
PACK = 4
ROWS = D // PACK
SIDE = P // ROWS
SETS = G // SIDE
HALF = N // 2
RUN = 4
MX_ALIGN = 64
DMA_ALIGN = 256
X_SPLIT = 304
EARLY = 2
R_LOADS = (EARLY, 2, 2, 1, 1)
STORES = (1,) * G


def interleave(copy, dst, src):
    copy(
        out=dst.rearrange("p (a b) j -> p a j b", b=RUN),
        in_=src.rearrange("p j (a b) -> p a j b", b=RUN),
    )


def batches(sizes):
    first = 0
    result = []
    for size in sizes:
        result.append(range(first, first + size))
        first = first + size
    return result


def tile_rows_glin_relu_res_kernel(tc, x, w, r, out):
    nc = tc.nc
    with ExitStack() as ctx:
        sb = ctx.enter_context(tc.tile_pool(name="sb", bufs=1))
        ps = ctx.enter_context(tc.psum_pool(name="ps", bufs=1))
        ctx.enter_context(tc.manual_schedule())

        w_raw = sb.tile([P, SETS, PACK, M], F32, name="w_raw", align_bytes=DMA_ALIGN)
        nc.sync.dma_start(
            out=w_raw[:].rearrange("p s j m -> p s (j m)"),
            in_=w.rearrange("(s c) (p j) m -> (c p) s (j m)", s=SETS, j=PACK),
        )

        def load_x(s):
            t = sb.tile([P, PACK, N], F32, name="x_raw%d" % s, align_bytes=DMA_ALIGN)
            nc.sync.dma_start(
                out=t[:].rearrange("p j n -> p (j n)"),
                in_=x[s * SIDE : (s + 1) * SIDE].rearrange("c (p j) n -> (c p) (j n)", j=PACK),
            )
            return t

        residual = {}

        def load_r(groups):
            t = sb.tile([P, len(groups), N], F32, name="r%d" % groups.start, align_bytes=DMA_ALIGN)
            nc.sync.dma_start(out=t[:], in_=r[groups.start : groups.stop].rearrange("g m n -> m g n"))
            for g in groups:
                residual[g] = t[:, g - groups.start, :]

        r_batches = batches(R_LOADS)
        x_raw = [load_x(0)]
        load_r(r_batches[0])
        x_raw.append(load_x(1))
        for groups in r_batches[1:]:
            load_r(groups)

        def quantize_halves(name, rounded):
            width = rounded[0].shape[1]
            codes = sb.tile([P, 2 * width], U32, name=name + "_codes", align_bytes=MX_ALIGN)
            scales = sb.tile([P, 2 * width], U8, name=name + "_scales", align_bytes=MX_ALIGN)
            for h, values in enumerate(rounded):
                cols = slice(h * width, (h + 1) * width)
                nc.vector.quantize_mx(
                    out=codes[:, cols].bitcast(FP8X4),
                    scales=scales[:, cols],
                    in_=values[:].rearrange("p n j -> p (n j)"),
                )
            return codes, scales

        w_bf = [sb.tile([P, M, PACK], BF16, name="w_bf%d" % s, align_bytes=MX_ALIGN) for s in range(SETS)]
        for s in range(SETS):
            interleave(nc.vector.tensor_copy, w_bf[s][:], w_raw[:, s])
        w_mx = quantize_halves("w", w_bf)

        acc = [ps.tile([M, N], F32, name="acc%d" % g) for g in range(G)]

        def round_x(s):
            lo = sb.tile([P, HALF, PACK], BF16, name="x_lo%d" % s, align_bytes=MX_ALIGN)
            hi = sb.tile([P, HALF, PACK], BF16, name="x_hi%d" % s, align_bytes=MX_ALIGN)
            interleave(nc.vector.tensor_copy, lo[:], x_raw[s][:, :, :HALF])
            interleave(nc.vector.tensor_copy, hi[:, : X_SPLIT - HALF, :], x_raw[s][:, :, HALF:X_SPLIT])
            interleave(nc.scalar.copy, hi[:, X_SPLIT - HALF :, :], x_raw[s][:, :, X_SPLIT:])
            return [lo, hi]

        def multiply_set(s, rounded):
            x_mx = quantize_halves("x%d" % s, rounded)
            cols = slice(s * M, (s + 1) * M)
            for c in range(SIDE):
                rows = slice(c * ROWS, (c + 1) * ROWS)
                nc.tensor.matmul_mx(
                    out=acc[s * SIDE + c][:],
                    lhsT=w_mx[0][rows, cols].bitcast(FP8X4),
                    lhsT_scale=w_mx[1][rows, cols],
                    rhs=x_mx[0][rows, :].bitcast(FP8X4),
                    rhs_scale=x_mx[1][rows, :],
                    start=True,
                    stop=True,
                )

        def finish(groups):
            y = sb.tile([P, len(groups), N], F32, name="y%d" % groups.start, align_bytes=DMA_ALIGN)
            for g in groups:
                nc.vector.scalar_tensor_tensor(
                    out=y[:, g - groups.start, :],
                    in0=acc[g][:],
                    scalar=0.0,
                    in1=residual[g],
                    op0=ALU.max,
                    op1=ALU.add,
                )
            return y

        def store(queue, groups, y):
            queue.dma_start(out=out[groups.start : groups.stop].rearrange("g m n -> m g n"), in_=y[:])

        stores = batches(STORES)
        multiply_set(0, round_x(0))
        store(nc.scalar, stores[0], finish(stores[0]))
        second = finish(stores[1])
        rounded = round_x(1)
        store(nc.scalar, stores[1], second)
        multiply_set(1, rounded)
        for groups in stores[EARLY:]:
            store(nc.sync, groups, finish(groups))
